import numpy as np
import ml_dtypes


def mxq(x, axis, fmt="e4m3"):
    dtype, down = {"e4m3": (ml_dtypes.float8_e4m3fn, 7), "e5m2": (ml_dtypes.float8_e5m2, 14)}[fmt]
    v = np.moveaxis(np.asarray(x, np.float32).astype(ml_dtypes.bfloat16).astype(np.float64), axis, -1)
    blocks = v.reshape(v.shape[:-1] + (-1, 32))
    amax = np.abs(blocks).max(-1, keepdims=True)
    byte = np.maximum(np.where(amax > 0, np.frexp(amax)[1] - 1 + 127, 0) - down, 1)
    scale = np.exp2(byte - 127.0)
    codes = (blocks / scale).astype(np.float32).astype(dtype).astype(np.float64)
    return np.moveaxis((codes * scale).reshape(v.shape), -1, axis)


WIDE = False


def mx_kscale(k):
    if not WIDE:
        return np.ones(k)
    levels = np.array([10, -10, 5, -5, 0])
    if k % 512:
        return np.exp2(np.random.permutation(np.resize(levels, k // 32))).repeat(32)
    a = np.empty((k // 512, 16))
    for p in range(k // 512):
        a[p, :8] = np.random.permutation(np.resize(levels, 8))
        for g in range(8):
            far = levels[np.abs(levels - a[p, g]) >= 10]
            a[p, g + 8] = far[np.random.randint(len(far))]
    return np.exp2(a.ravel()).repeat(32)


def f64(x):
    return np.asarray(x).astype(np.float64)


def striped(idx):
    return np.tile(idx.reshape(-1, 16).T, (8, 1)).astype(np.uint16)


def unstriped(offs):
    return offs[:16].T.reshape(-1).astype(np.int64)


E2M1 = np.array([0.0, 0.5, 1.0, 1.5, 2.0, 3.0, 4.0, 6.0, -0.0, -0.5, -1.0, -1.5, -2.0, -3.0, -4.0, -6.0])


def pack_weight(w, fmt):
    k, n = w.shape
    w = f64(np.asarray(w, np.float32).astype(ml_dtypes.bfloat16)).reshape(k // 32, 32, n)
    amax = np.abs(w).max(1)
    if fmt == "e4m3":
        byte = np.frexp(amax)[1] - 1 + 127 - 7
    else:
        mant, ex = np.frexp(amax / 6.0)
        byte = np.where(mant > 0.5, ex, ex - 1) + 127
    byte = np.clip(np.where(amax > 0, byte, 1), 1, 254)
    scaled = (w * np.exp2(127.0 - byte)[:, None, :]).reshape(k, n).astype(np.float32)
    by_word = np.ascontiguousarray(scaled.reshape(k // 512, 128, 4, n).transpose(0, 1, 3, 2))
    if fmt == "e4m3":
        words = by_word.astype(ml_dtypes.float8_e4m3fn).view(np.uint8)
    else:
        c = by_word.astype(ml_dtypes.float4_e2m1fn).view(np.uint8) & 0xF
        words = (c[..., 0::2] | (c[..., 1::2] << 4)).reshape(k // 512, 128, 2 * n)
    return np.ascontiguousarray(words), np.ascontiguousarray(byte.astype(np.uint8).reshape(k // 512, 16, n))


def unpack_weight(words, scales, fmt):
    g, _, n = scales.shape
    words = np.ascontiguousarray(words).reshape(g, 128, n, -1)
    if fmt == "e4m3":
        vals = words.view(ml_dtypes.float8_e4m3fn).astype(np.float64)
    else:
        nib = np.empty((g, 128, n, 4), np.uint8)
        nib[..., 0::2] = words & 0xF
        nib[..., 1::2] = words >> 4
        vals = E2M1[nib]
    vals = vals * np.repeat(np.exp2(scales.astype(np.float64) - 127.0), 8, axis=1)[..., None]
    return vals.transpose(0, 1, 3, 2).reshape(g * 512, n)


def relu(v):
    return np.maximum(v, 0.0)


K, T, E, C, H, N, TOP = 512, 640, 10, 256, 512, 128, 4


def by_expert(wq, xq):
    return np.concatenate([wq[e].T @ xq[:, e * C:(e + 1) * C] for e in range(E)], axis=1)


def setup_inputs():
    n = np.random.standard_normal
    s = mx_kscale(K)
    u = mx_kscale(H)
    deal = np.repeat(np.arange(E), C).reshape(TOP, T)[:, np.random.permutation(T)]
    deal = np.take_along_axis(deal, np.argsort(np.random.rand(TOP, T), axis=0), axis=0)
    for _ in range(8):
        s_, t_ = np.random.permutation(T).reshape(2, -1); r = np.random.randint(TOP, size=T // 2); x, y = deal[r, s_].copy(), deal[r, t_].copy()
        ok = ~((deal[:, s_] == y).any(0) | (deal[:, t_] == x).any(0)); deal[r[ok], s_[ok]] = y[ok]; deal[r[ok], t_[ok]] = x[ok]
    order = np.lexsort((np.random.rand(TOP * T), deal.reshape(-1)))
    slot_token = order % T; pos = np.empty(TOP * T, np.int64); pos[order] = np.arange(TOP * T); pos = pos.reshape(TOP, T)
    g = np.random.uniform(0.5, 1.5, (TOP, T)); g = g / g.sum(0)
    x = pack_weight(n((K, T)) * s[:, None], "e4m3")
    w1 = pack_weight(n((K, H)) / np.sqrt(K) / s[:, None] * u, "e2m1")
    w2 = [pack_weight(m, "e4m3") for m in n((E, H, N)) / np.sqrt(H) / u[None, :, None]]
    return {
        "x_words": x[0],
        "x_scales": x[1],
        "w1_words": w1[0],
        "w1_scales": w1[1],
        "w2_words": np.stack([m[0] for m in w2]),
        "w2_scales": np.stack([m[1] for m in w2]),
        "gate": np.stack([np.tile(r, (128, 1)) for r in g]).astype(np.float32),
        "offs": striped(slot_token),
        "pos1": striped(pos[0]),
        "pos2": striped(pos[1]),
        "pos3": striped(pos[2]),
        "pos4": striped(pos[3]),
    }


def reference(x_words, x_scales, w1_words, w1_scales, w2_words, w2_scales, gate, offs, pos1, pos2, pos3, pos4):
    w1 = unpack_weight(w1_words, w1_scales, "e2m1")
    w2 = np.stack([unpack_weight(w2_words[e], w2_scales[e], "e4m3") for e in range(E)])
    idx = unstriped(offs)
    x = unpack_weight(x_words, x_scales, "e4m3")
    h = relu(w1.T @ x)
    y = by_expert(w2, mxq(h[:, idx], 0, "e4m3"))
    out = sum(f64(gate[r, :1]) * y[:, unstriped(p)] for r, p in enumerate((pos1, pos2, pos3, pos4)))
    return out

@@ -1,0 +1,195 @@
+from contextlib import ExitStack
+
+import concourse.mybir as mybir
+
+K, T, E, C, H, N, TOP = 512, 640, 10, 256, 512, 128, 4
+S = E * C
+FLOPS = 2 * K * H * T + 2 * H * N * S
+
+F32 = mybir.dt.float32
+BF16 = mybir.dt.bfloat16
+I32 = mybir.dt.int32
+U32 = mybir.dt.uint32
+U16 = mybir.dt.uint16
+U8 = mybir.dt.uint8
+FP8X4 = mybir.dt.float8_e4m3fn_x4
+FP4X4 = mybir.dt.float4_e2m1fn_x4
+MULT = mybir.AluOpType.mult
+ADD = mybir.AluOpType.add
+MAX = mybir.AluOpType.max
+RELU = mybir.ActivationFunctionType.Relu
+
+P = 128
+T_WIN = 704
+TOKEN_CHUNKS = ((0, 256), (256, 256), (512, 128))
+SLOT_PIECES = ((0, 512), (512, 512), (1024, 512), (1536, 512), (2048, 256), (2304, 128), (2432, 128))
+
+
+def tile_moe_sup_lin_relu_kernel(
+    tc, x_words, x_scales, w1_words, w1_scales, w2_words, w2_scales, gate, offs, pos1, pos2, pos3, pos4, out
+):
+    nc = tc.nc
+    with ExitStack() as ctx:
+        lists = ctx.enter_context(tc.tile_pool(name="lists", bufs=1))
+        keep = ctx.enter_context(tc.tile_pool(name="keep", bufs=1))
+        ring = ctx.enter_context(tc.tile_pool(name="ring", bufs=3))
+        psum1 = ctx.enter_context(tc.psum_pool(name="psum1", bufs=1))
+        psum2 = ctx.enter_context(tc.psum_pool(name="psum2", bufs=2))
+
+        offs_sb = lists.tile([P, S // 16], U16, name="offs_sb")
+        pos_sb = [lists.tile([P, T // 16], U16, name="pos_sb%d" % r) for r in range(TOP)]
+
+        xw = keep.tile([P, T], U32, name="xw", align_bytes=64)
+        xs = keep.tile([P, T], U8, name="xs", align_bytes=64)
+        w1w_raw = keep.tile([P, 2 * H], U8, name="w1w_raw", align_bytes=64)
+        w1s_raw = keep.tile([P, H], U8, name="w1s_raw", align_bytes=64)
+        w1w = keep.tile([P, 2 * H], U8, name="w1w", align_bytes=64)
+        w1s = keep.tile([P, H], U8, name="w1s", align_bytes=64)
+        w2w = keep.tile([P, E, N], U32, name="w2w", align_bytes=64)
+        w2s = keep.tile([P, E, N], U8, name="w2s", align_bytes=64)
+        gates = keep.tile([P, TOP, T], F32, name="gates", align_bytes=64)
+        hp = [keep.tile([P, T_WIN, 2], BF16, name="hp%d" % u, align_bytes=64) for u in range(2)]
+        y = keep.tile([P, S], F32, name="y", align_bytes=64)
+        warm_in = keep.tile([P, 1], F32, name="warm_in")
+        warm_out = keep.tile([P, 1], F32, name="warm_out")
+
+        nc.vector.memset(w1s_raw[:].bitcast(I32), 0)
+        nc.vector.memset(xs[:].bitcast(I32), 0)
+        nc.vector.memset(warm_in[:], 0.0)
+        nc.vector.memset(w2s[:].rearrange("p e n -> p (e n)").bitcast(I32), 0)
+        for u in range(2):
+            nc.vector.memset(hp[u][:, T:T_WIN, :], 0.0)
+        nc.scalar.activation(warm_out[:], warm_in[:], RELU)
+
+        def load_scale_rows(dst, src, q):
+            nc.sync.dma_start(dst[32 * q : 32 * q + 4, :].bitcast(I32), src[4 * q : 4 * q + 4, :].bitcast(I32))
+
+        nc.sync.dma_start(offs_sb[:], offs)
+        for q in range(4):
+            load_scale_rows(w1s_raw, w1_scales[0], q)
+        nc.sync.dma_start(w1w_raw[:].bitcast(I32), w1_words[0].bitcast(I32))
+        load_scale_rows(xs, x_scales[0], 0)
+        nc.sync.dma_start(xw[:].bitcast(I32), x_words[0].rearrange("p t d -> p (t d)").bitcast(I32))
+        for q in range(1, 4):
+            load_scale_rows(xs, x_scales[0], q)
+        for q in range(4):
+            nc.sync.dma_start(
+                w2s[32 * q : 32 * q + 4, :, :].bitcast(I32),
+                w2_scales[:, 0, 4 * q : 4 * q + 4, :].rearrange("e r n -> r e n").bitcast(I32),
+            )
+        nc.sync.dma_start(
+            w2w[:].bitcast(I32), w2_words[:, 0].rearrange("e p n d -> p e (n d)").bitcast(I32)
+        )
+        for r, pos in enumerate((pos1, pos2, pos3, pos4)):
+            nc.sync.dma_start(pos_sb[r][:], pos)
+        nc.sync.dma_start(gates[:], gate.rearrange("r p t -> p r t"))
+
+        for u in range(2):
+            planes = slice(2 * u, 2 * u + 2)
+            nc.vector.tensor_copy(
+                w1s[:].rearrange("p (j m) -> p j m", j=4)[:, planes, :],
+                w1s_raw[:].rearrange("p (m j) -> p j m", j=4)[:, planes, :],
+            )
+            nc.vector.tensor_copy(
+                w1w[:].bitcast(U16).rearrange("p (j m) -> p j m", j=4)[:, planes, :],
+                w1w_raw[:].bitcast(U16).rearrange("p (m j) -> p j m", j=4)[:, planes, :],
+            )
+        for u in range(2):
+            for c, (t0, n) in enumerate(TOKEN_CHUNKS):
+                bank = psum1.tile([P, 2, n], F32, name="h_bank%d%d" % (u, c))
+                for e in range(2):
+                    j = 2 * u + e
+                    nc.tensor.matmul_mx(
+                        out=bank[:, e, :],
+                        lhsT=w1w[:, 2 * P * j : 2 * P * (j + 1)].bitcast(FP4X4),
+                        lhsT_scale=w1s[:, P * j : P * (j + 1)],
+                        rhs=xw[:, t0 : t0 + n].bitcast(FP8X4),
+                        rhs_scale=xs[:, t0 : t0 + n],
+                        start=True,
+                        stop=True,
+                    )
+                src = bank[:].rearrange("p e t -> p t e")
+                dst = hp[u][:, t0 : t0 + n, :]
+                if u == 0 and c != 1:
+                    nc.vector.tensor_scalar(dst, src, 0.0, None, MAX)
+                else:
+                    nc.scalar.activation(dst, src, RELU)
+
+        halves = {}
+        rows4 = [keep.tile([P, n * 4], BF16, name="rows4_%d" % i, align_bytes=64) for i, (s0, n) in enumerate(SLOT_PIECES)]
+        codes = [keep.tile([P, n], U32, name="codes%d" % i, align_bytes=64) for i, (s0, n) in enumerate(SLOT_PIECES)]
+        scales = [keep.tile([P, n], U8, name="scales%d" % i, align_bytes=64) for i, (s0, n) in enumerate(SLOT_PIECES)]
+
+        def gather(i, u):
+            s0, n = SLOT_PIECES[i]
+            if i not in halves:
+                halves.setdefault(i, ring.tile([P, 2, n], U32, name="halves", align_bytes=64))
+            window = hp[u][:].rearrange("p t e -> p (t e)").bitcast(U32)
+            nc.vector.tensor_copy(halves[i][:, u, :], window.indirect(offs_sb[:, s0 // 16 : (s0 + n) // 16]))
+
+        def interleave(i):
+            nc.scalar.copy(
+                rows4[i][:].bitcast(F32).rearrange("p (s u) -> p s u", u=2),
+                halves[i][:].bitcast(F32).rearrange("p u s -> p s u"),
+            )
+
+        def second_layer(i):
+            s0, n = SLOT_PIECES[i]
+            nc.vector.quantize_mx(out=codes[i][:].bitcast(FP8X4), scales=scales[i][:], in_=rows4[i][:])
+            bank = psum2.tile([P, 512], F32, name="y_bank")
+            width = min(n, C)
+            for a in range(0, n, width):
+                e = (s0 + a) // C
+                nc.tensor.matmul_mx(
+                    out=bank[:, a : a + width],
+                    lhsT=w2w[:, e, :].bitcast(FP8X4),
+                    lhsT_scale=w2s[:, e, :],
+                    rhs=codes[i][:, a : a + width].bitcast(FP8X4),
+                    rhs_scale=scales[i][:, a : a + width],
+                    start=True,
+                    stop=True,
+                )
+            nc.scalar.copy(y[:, s0 : s0 + n], bank[:, 0:n])
+
+        gather(0, 0)
+        gather(1, 0)
+        gather(0, 1)
+        interleave(0)
+        gather(1, 1)
+        interleave(1)
+        for i in range(2, len(SLOT_PIECES)):
+            gather(i, 0)
+            gather(i, 1)
+            interleave(i)
+            second_layer(i - 2)
+        second_layer(len(SLOT_PIECES) - 2)
+        second_layer(len(SLOT_PIECES) - 1)
+
+        TA = 512
+        TB = T - TA
+        pa = keep.tile([P, TOP, TA], F32, name="pa", align_bytes=64)
+        pb = keep.tile([P, TOP, TB], F32, name="pb", align_bytes=64)
+        sa2 = keep.tile([P, 2, TA], F32, name="sa2", align_bytes=64)
+        sa = keep.tile([P, TA], F32, name="sa", align_bytes=64)
+        sb01 = keep.tile([P, TB], F32, name="sb01", align_bytes=64)
+        sb012 = keep.tile([P, TB], F32, name="sb012", align_bytes=64)
+        sb = keep.tile([P, TB], F32, name="sb", align_bytes=64)
+
+        def fetch(dst, r, t0, n):
+            nc.vector.tensor_tensor(
+                dst[:, r, :], y[:].indirect(pos_sb[r][:, t0 // 16 : (t0 + n) // 16]), gates[:, r, t0 : t0 + n], MULT
+            )
+
+        for r in range(TOP):
+            fetch(pa, r, 0, TA)
+        fetch(pb, 0, TA, TB)
+        nc.vector.tensor_tensor(sa2[:], pa[:, 0:2, :], pa[:, 2:4, :], ADD)
+        fetch(pb, 1, TA, TB)
+        nc.vector.tensor_tensor(sa[:], sa2[:, 0, :], sa2[:, 1, :], ADD)
+        nc.sync.dma_start(out[:, 0:TA], sa[:])
+        fetch(pb, 2, TA, TB)
+        nc.vector.tensor_tensor(sb01[:], pb[:, 0, :], pb[:, 1, :], ADD)
+        fetch(pb, 3, TA, TB)
+        nc.vector.tensor_tensor(sb012[:], sb01[:], pb[:, 2, :], ADD)
+        nc.vector.tensor_tensor(sb[:], sb012[:], pb[:, 3, :], ADD)
+        nc.sync.dma_start(out[:, TA:T], sb[:])

@@ -1,6 +1,7 @@
 from contextlib import ExitStack
 
 import concourse.mybir as mybir
+from concourse.masks import make_identity
 
 K, T, E, C, H, N, TOP = 512, 640, 10, 256, 512, 128, 4
 S = E * C
@@ -22,7 +23,7 @@ RELU = mybir.ActivationFunctionType.Relu
 P = 128
 T_WIN = 704
 TOKEN_CHUNKS = ((0, 256), (256, 256), (512, 128))
-SLOT_PIECES = ((0, 512), (512, 512), (1024, 512), (1536, 512), (2048, 256), (2304, 128), (2432, 128))
+SLOT_PIECES = ((0, 256), (256, 512), (768, 512), (1280, 512), (1792, 256), (2048, 256), (2304, 128), (2432, 128))
 
 
 def tile_moe_sup_lin_relu_kernel(
@@ -32,9 +33,8 @@ def tile_moe_sup_lin_relu_kernel(
     with ExitStack() as ctx:
         lists = ctx.enter_context(tc.tile_pool(name="lists", bufs=1))
         keep = ctx.enter_context(tc.tile_pool(name="keep", bufs=1))
-        ring = ctx.enter_context(tc.tile_pool(name="ring", bufs=3))
-        psum1 = ctx.enter_context(tc.psum_pool(name="psum1", bufs=1))
-        psum2 = ctx.enter_context(tc.psum_pool(name="psum2", bufs=2))
+        ring = ctx.enter_context(tc.tile_pool(name="ring", bufs=2))
+        psum = ctx.enter_context(tc.psum_pool(name="psum", bufs=1))
 
         offs_sb = lists.tile([P, S // 16], U16, name="offs_sb")
         pos_sb = [lists.tile([P, T // 16], U16, name="pos_sb%d" % r) for r in range(TOP)]
@@ -60,6 +60,9 @@ def tile_moe_sup_lin_relu_kernel(
         for u in range(2):
             nc.vector.memset(hp[u][:, T:T_WIN, :], 0.0)
         nc.scalar.activation(warm_out[:], warm_in[:], RELU)
+        ident = keep.tile([P, P], F32, name="ident", align_bytes=64)
+        nc.vector.memset(ident[:], 0.0)
+        make_identity(nc, ident[:], nomemset=True)
 
         def load_scale_rows(dst, src, q):
             nc.sync.dma_start(dst[32 * q : 32 * q + 4, :].bitcast(I32), src[4 * q : 4 * q + 4, :].bitcast(I32))
@@ -96,7 +99,7 @@ def tile_moe_sup_lin_relu_kernel(
             )
         for u in range(2):
             for c, (t0, n) in enumerate(TOKEN_CHUNKS):
-                bank = psum1.tile([P, 2, n], F32, name="h_bank%d%d" % (u, c))
+                bank = psum.tile([P, 2, n], F32, name="h_bank%d%d" % (u, c), tag="bank%d" % (3 * u + c))
                 for e in range(2):
                     j = 2 * u + e
                     nc.tensor.matmul_mx(
@@ -133,10 +136,12 @@ def tile_moe_sup_lin_relu_kernel(
                 halves[i][:].bitcast(F32).rearrange("p u s -> p s u"),
             )
 
+        y_banks = {}
+
         def second_layer(i):
             s0, n = SLOT_PIECES[i]
             nc.vector.quantize_mx(out=codes[i][:].bitcast(FP8X4), scales=scales[i][:], in_=rows4[i][:])
-            bank = psum2.tile([P, 512], F32, name="y_bank")
+            bank = y_banks.setdefault(i, psum.tile([P, n], F32, name="y_bank%d" % i, tag="bank%d" % ((6 + i) % 8)))
             width = min(n, C)
             for a in range(0, n, width):
                 e = (s0 + a) // C
@@ -149,7 +154,15 @@ def tile_moe_sup_lin_relu_kernel(
                     start=True,
                     stop=True,
                 )
-            nc.scalar.copy(y[:, s0 : s0 + n], bank[:, 0:n])
+
+        def empty(i):
+            s0, n = SLOT_PIECES[i]
+            nc.scalar.copy(y[:, s0 : s0 + n], y_banks[i][:])
+
+        def bring(i):
+            gather(i, 0)
+            gather(i, 1)
+            interleave(i)
 
         gather(0, 0)
         gather(1, 0)
@@ -157,39 +170,78 @@ def tile_moe_sup_lin_relu_kernel(
         interleave(0)
         gather(1, 1)
         interleave(1)
-        for i in range(2, len(SLOT_PIECES)):
-            gather(i, 0)
-            gather(i, 1)
-            interleave(i)
-            second_layer(i - 2)
-        second_layer(len(SLOT_PIECES) - 2)
-        second_layer(len(SLOT_PIECES) - 1)
+        second_layer(0)
+        empty(0)
+        for i in (2, 3):
+            bring(i)
+            second_layer(i - 1)
+            empty(i - 1)
+        bring(4)
+        second_layer(3)
+        bring(5)
+        second_layer(4)
+        empty(3)
+        bring(6)
+        bring(7)
+        for i in (5, 6, 7):
+            second_layer(i)
+        for i in (4, 5, 6, 7):
+            empty(i)
 
-        TA = 512
+        TA = 384
         TB = T - TA
-        pa = keep.tile([P, TOP, TA], F32, name="pa", align_bytes=64)
-        pb = keep.tile([P, TOP, TB], F32, name="pb", align_bytes=64)
-        sa2 = keep.tile([P, 2, TA], F32, name="sa2", align_bytes=64)
-        sa = keep.tile([P, TA], F32, name="sa", align_bytes=64)
-        sb01 = keep.tile([P, TB], F32, name="sb01", align_bytes=64)
-        sb012 = keep.tile([P, TB], F32, name="sb012", align_bytes=64)
-        sb = keep.tile([P, TB], F32, name="sb", align_bytes=64)
+        prod = keep.tile([P, TOP, T], F32, name="prod", align_bytes=64)
+        turned = keep.tile([P, TA // P, P], F32, name="turned", align_bytes=64)
+        res_a = keep.tile([P, TA], F32, name="res_a", align_bytes=64)
+        res_b = keep.tile([P, TB], F32, name="res_b", align_bytes=64)
+        s01 = keep.tile([P, TB], F32, name="s01", align_bytes=64)
+        s012 = keep.tile([P, TB], F32, name="s012", align_bytes=64)
+        sums = [psum.tile([P, P], F32, name="sum%d" % b, tag="bank%d" % ((6 + b) % 8)) for b in range(TA // P)]
+        back = psum.tile([P, TA], F32, name="back", tag="bank1")
 
-        def fetch(dst, r, t0, n):
+        def fetch(r, t0, n):
             nc.vector.tensor_tensor(
-                dst[:, r, :], y[:].indirect(pos_sb[r][:, t0 // 16 : (t0 + n) // 16]), gates[:, r, t0 : t0 + n], MULT
+                prod[:, r, t0 : t0 + n],
+                y[:].indirect(pos_sb[r][:, t0 // 16 : (t0 + n) // 16]),
+                gates[:, r, t0 : t0 + n],
+                MULT,
             )
 
         for r in range(TOP):
-            fetch(pa, r, 0, TA)
-        fetch(pb, 0, TA, TB)
-        nc.vector.tensor_tensor(sa2[:], pa[:, 0:2, :], pa[:, 2:4, :], ADD)
-        fetch(pb, 1, TA, TB)
-        nc.vector.tensor_tensor(sa[:], sa2[:, 0, :], sa2[:, 1, :], ADD)
-        nc.sync.dma_start(out[:, 0:TA], sa[:])
-        fetch(pb, 2, TA, TB)
-        nc.vector.tensor_tensor(sb01[:], pb[:, 0, :], pb[:, 1, :], ADD)
-        fetch(pb, 3, TA, TB)
-        nc.vector.tensor_tensor(sb012[:], sb01[:], pb[:, 2, :], ADD)
-        nc.vector.tensor_tensor(sb[:], sb012[:], pb[:, 3, :], ADD)
-        nc.sync.dma_start(out[:, TA:T], sb[:])
+            fetch(r, 0, TA)
+            for b in range(TA // P):
+                nc.tensor.matmul(
+                    sums[b][:],
+                    lhsT=prod[:, r, P * b : P * (b + 1)],
+                    rhs=ident[:],
+                    start=(r == 0),
+                    stop=(r == TOP - 1),
+                    is_transpose=True,
+                )
+        for b in range(TA // P):
+            nc.scalar.copy(turned[:, b, :], sums[b][:])
+            nc.tensor.transpose(back[:, P * b : P * (b + 1)], turned[:, b, :], ident[:])
+        nc.scalar.copy(res_a[:], back[:])
+        nc.sync.dma_start(out[:, 0:TA], res_a[:])
+
+        def add(dst, left, r, t0):
+            a = t0 - TA
+            nc.vector.tensor_tensor(dst[:, a : a + P], left, prod[:, r, t0 : t0 + P], ADD)
+
+        td, tcc = TA, TA + P
+        fetch(0, td, P)
+        fetch(1, td, P)
+        fetch(0, tcc, P)
+        fetch(1, tcc, P)
+        add(s01, prod[:, 0, td : td + P], 1, td)
+        fetch(2, td, P)
+        add(s01, prod[:, 0, tcc : tcc + P], 1, tcc)
+        fetch(2, tcc, P)
+        fetch(3, td, P)
+        add(s012, s01[:, 0:P], 2, td)
+        add(s012, s01[:, P : 2 * P], 2, tcc)
+        add(res_b, s012[:, 0:P], 3, td)
+        nc.sync.dma_start(out[:, td : td + P], res_b[:, 0:P])
+        fetch(3, tcc, P)
+        add(res_b, s012[:, P : 2 * P], 3, tcc)
+        nc.sync.dma_start(out[:, tcc : tcc + P], res_b[:, P : 2 * P])

@@ -19,11 +19,14 @@ MULT = mybir.AluOpType.mult
 ADD = mybir.AluOpType.add
 MAX = mybir.AluOpType.max
 RELU = mybir.ActivationFunctionType.Relu
+COPY = mybir.ActivationFunctionType.Copy
 
 P = 128
 T_WIN = 704
 TOKEN_CHUNKS = ((0, 256), (256, 256), (512, 128))
 SLOT_PIECES = ((0, 256), (256, 512), (768, 512), (1280, 512), (1792, 256), (2048, 256), (2304, 128), (2432, 128))
+SHARED_PIECES = (5, 6)
+BANK_OF_PIECE = {0: 6, 1: 7, 2: 0, 5: 1, 3: 2, 6: 3, 4: 4, 7: 5}
 
 
 def tile_moe_sup_lin_relu_kernel(
@@ -97,9 +100,12 @@ def tile_moe_sup_lin_relu_kernel(
                 w1w[:].bitcast(U16).rearrange("p (j m) -> p j m", j=4)[:, planes, :],
                 w1w_raw[:].bitcast(U16).rearrange("p (m j) -> p j m", j=4)[:, planes, :],
             )
+        h_banks = {}
         for u in range(2):
             for c, (t0, n) in enumerate(TOKEN_CHUNKS):
-                bank = psum.tile([P, 2, n], F32, name="h_bank%d%d" % (u, c), tag="bank%d" % (3 * u + c))
+                bank = h_banks.setdefault(
+                    (u, c), psum.tile([P, 2, n], F32, name="h_bank%d%d" % (u, c), tag="bank%d" % (3 * u + c))
+                )
                 for e in range(2):
                     j = 2 * u + e
                     nc.tensor.matmul_mx(
@@ -118,7 +124,14 @@ def tile_moe_sup_lin_relu_kernel(
                 else:
                     nc.scalar.activation(dst, src, RELU)
 
-        halves = {}
+        rows23 = keep.tile([P, 2, T], BF16, name="rows23", align_bytes=64)
+        for c, (t0, n) in enumerate(TOKEN_CHUNKS):
+            nc.scalar.activation(rows23[:, :, t0 : t0 + n], h_banks[(1, c)][:], RELU)
+
+        halves = {
+            i: keep.tile([P, 2, SLOT_PIECES[i][1]], U32, name="halves_shared%d" % i, align_bytes=64)
+            for i in SHARED_PIECES
+        }
         rows4 = [keep.tile([P, n * 4], BF16, name="rows4_%d" % i, align_bytes=64) for i, (s0, n) in enumerate(SLOT_PIECES)]
         codes = [keep.tile([P, n], U32, name="codes%d" % i, align_bytes=64) for i, (s0, n) in enumerate(SLOT_PIECES)]
         scales = [keep.tile([P, n], U8, name="scales%d" % i, align_bytes=64) for i, (s0, n) in enumerate(SLOT_PIECES)]
@@ -129,6 +142,14 @@ def tile_moe_sup_lin_relu_kernel(
                 halves.setdefault(i, ring.tile([P, 2, n], U32, name="halves", align_bytes=64))
             window = hp[u][:].rearrange("p t e -> p (t e)").bitcast(U32)
             nc.vector.tensor_copy(halves[i][:, u, :], window.indirect(offs_sb[:, s0 // 16 : (s0 + n) // 16]))
+
+        def gather_on_scalar(i, e):
+            s0, n = SLOT_PIECES[i]
+            nc.scalar.activation(
+                halves[i][:, 1, :].bitcast(BF16).rearrange("p (s e) -> p s e", e=2)[:, :, e],
+                rows23[:, e, :].indirect(offs_sb[:, s0 // 16 : (s0 + n) // 16]),
+                COPY,
+            )
 
         def interleave(i):
             nc.scalar.copy(
@@ -141,7 +162,7 @@ def tile_moe_sup_lin_relu_kernel(
         def second_layer(i):
             s0, n = SLOT_PIECES[i]
             nc.vector.quantize_mx(out=codes[i][:].bitcast(FP8X4), scales=scales[i][:], in_=rows4[i][:])
-            bank = y_banks.setdefault(i, psum.tile([P, n], F32, name="y_bank%d" % i, tag="bank%d" % ((6 + i) % 8)))
+            bank = y_banks.setdefault(i, psum.tile([P, n], F32, name="y_bank%d" % i, tag="bank%d" % BANK_OF_PIECE[i]))
             width = min(n, C)
             for a in range(0, n, width):
                 e = (s0 + a) // C
@@ -157,7 +178,10 @@ def tile_moe_sup_lin_relu_kernel(
 
         def empty(i):
             s0, n = SLOT_PIECES[i]
-            nc.scalar.copy(y[:, s0 : s0 + n], y_banks[i][:])
+            if i == 4:
+                nc.vector.tensor_copy(y[:, s0 : s0 + n], y_banks[i][:])
+            else:
+                nc.scalar.copy(y[:, s0 : s0 + n], y_banks[i][:])
 
         def bring(i):
             gather(i, 0)
@@ -166,26 +190,35 @@ def tile_moe_sup_lin_relu_kernel(
 
         gather(0, 0)
         gather(1, 0)
+        gather(5, 0)
+        gather(6, 0)
         gather(0, 1)
+        gather_on_scalar(5, 0)
         interleave(0)
         gather(1, 1)
         interleave(1)
         second_layer(0)
         empty(0)
-        for i in (2, 3):
-            bring(i)
-            second_layer(i - 1)
-            empty(i - 1)
+        gather_on_scalar(5, 1)
+        bring(2)
+        second_layer(1)
+        interleave(5)
+        empty(1)
+        gather_on_scalar(6, 0)
+        gather_on_scalar(6, 1)
+        bring(3)
+        second_layer(2)
+        interleave(6)
+        empty(2)
         bring(4)
+        second_layer(5)
         second_layer(3)
-        bring(5)
-        second_layer(4)
-        empty(3)
-        bring(6)
+        empty(5)
         bring(7)
-        for i in (5, 6, 7):
-            second_layer(i)
-        for i in (4, 5, 6, 7):
+        second_layer(6)
+        second_layer(4)
+        second_layer(7)
+        for i in (3, 6, 4, 7):
             empty(i)
 
         TA = 384

@@ -24,9 +24,9 @@ COPY = mybir.ActivationFunctionType.Copy
 P = 128
 T_WIN = 704
 TOKEN_CHUNKS = ((0, 256), (256, 256), (512, 128))
-SLOT_PIECES = ((0, 256), (256, 512), (768, 512), (1280, 512), (1792, 256), (2048, 256), (2304, 128), (2432, 128))
+SLOT_PIECES = ((0, 256), (256, 512), (768, 512), (1280, 512), (1792, 128), (2048, 256), (2304, 256), (1920, 128))
 SHARED_PIECES = (5, 6)
-BANK_OF_PIECE = {0: 6, 1: 7, 2: 0, 5: 1, 3: 2, 6: 3, 4: 4, 7: 5}
+BANK_OF_PIECE = {0: 6, 1: 7, 5: 0, 2: 1, 3: 2, 6: 3, 4: 4, 7: 5}
 
 
 def tile_moe_sup_lin_relu_kernel(
@@ -70,14 +70,15 @@ def tile_moe_sup_lin_relu_kernel(
         def load_scale_rows(dst, src, q):
             nc.sync.dma_start(dst[32 * q : 32 * q + 4, :].bitcast(I32), src[4 * q : 4 * q + 4, :].bitcast(I32))
 
-        nc.sync.dma_start(offs_sb[:], offs)
+        nc.sync.dma_start(w1w_raw[:].bitcast(I32), w1_words[0].bitcast(I32))
         for q in range(4):
             load_scale_rows(w1s_raw, w1_scales[0], q)
-        nc.sync.dma_start(w1w_raw[:].bitcast(I32), w1_words[0].bitcast(I32))
-        load_scale_rows(xs, x_scales[0], 0)
-        nc.sync.dma_start(xw[:].bitcast(I32), x_words[0].rearrange("p t d -> p (t d)").bitcast(I32))
-        for q in range(1, 4):
+        for q in range(2):
             load_scale_rows(xs, x_scales[0], q)
+        nc.sync.dma_start(xw[:].bitcast(I32), x_words[0].rearrange("p t d -> p (t d)").bitcast(I32))
+        for q in range(2, 4):
+            load_scale_rows(xs, x_scales[0], q)
+        nc.sync.dma_start(offs_sb[:], offs)
         for q in range(4):
             nc.sync.dma_start(
                 w2s[32 * q : 32 * q + 4, :, :].bitcast(I32),
@@ -195,25 +196,25 @@ def tile_moe_sup_lin_relu_kernel(
         gather(0, 1)
         gather_on_scalar(5, 0)
         interleave(0)
+        gather_on_scalar(5, 1)
         gather(1, 1)
         interleave(1)
         second_layer(0)
         empty(0)
-        gather_on_scalar(5, 1)
+        gather_on_scalar(6, 0)
+        interleave(5)
         bring(2)
         second_layer(1)
-        interleave(5)
-        empty(1)
-        gather_on_scalar(6, 0)
         gather_on_scalar(6, 1)
+        empty(1)
         bring(3)
+        second_layer(5)
         second_layer(2)
         interleave(6)
+        empty(5)
         empty(2)
         bring(4)
-        second_layer(5)
         second_layer(3)
-        empty(5)
         bring(7)
         second_layer(6)
         second_layer(4)

@@ -24,9 +24,13 @@ COPY = mybir.ActivationFunctionType.Copy
 P = 128
 T_WIN = 704
 TOKEN_CHUNKS = ((0, 256), (256, 256), (512, 128))
-SLOT_PIECES = ((0, 256), (256, 512), (768, 512), (1280, 512), (1792, 128), (2048, 256), (2304, 256), (1920, 128))
-SHARED_PIECES = (5, 6)
-BANK_OF_PIECE = {0: 6, 1: 7, 5: 0, 2: 1, 3: 2, 6: 3, 4: 4, 7: 5}
+PIECES = ((0, 256, 0), (256, 512, 0), (768, 512, 352), (1280, 512, 352), (1792, 512, 352), (2304, 256, 0))
+LAST = len(PIECES) - 1
+WIDE = 512
+G_SLOTS = 320
+Y_BANK = {0: 6, 1: 7, 3: 0, 5: 1, 7: 2, 8: 3, 9: 4}
+SUM_BANKS = (5, 6, 7, 0, 1)
+BACK_BANKS = (2, 3, 4)
 
 
 def tile_moe_sup_lin_relu_kernel(
@@ -126,112 +130,103 @@ def tile_moe_sup_lin_relu_kernel(
                     nc.scalar.activation(dst, src, RELU)
 
         rows23 = keep.tile([P, 2, T], BF16, name="rows23", align_bytes=64)
-        for c, (t0, n) in enumerate(TOKEN_CHUNKS):
-            nc.scalar.activation(rows23[:, :, t0 : t0 + n], h_banks[(1, c)][:], RELU)
+        for t0, n in TOKEN_CHUNKS:
+            nc.gpsimd.tensor_copy(rows23[:, :, t0 : t0 + n], hp[1][:, t0 : t0 + n, :].rearrange("p t e -> p e t"))
 
-        halves = {
-            i: keep.tile([P, 2, SLOT_PIECES[i][1]], U32, name="halves_shared%d" % i, align_bytes=64)
-            for i in SHARED_PIECES
-        }
-        rows4 = [keep.tile([P, n * 4], BF16, name="rows4_%d" % i, align_bytes=64) for i, (s0, n) in enumerate(SLOT_PIECES)]
-        codes = [keep.tile([P, n], U32, name="codes%d" % i, align_bytes=64) for i, (s0, n) in enumerate(SLOT_PIECES)]
-        scales = [keep.tile([P, n], U8, name="scales%d" % i, align_bytes=64) for i, (s0, n) in enumerate(SLOT_PIECES)]
+        halves = {}
+        arena = keep.tile([P, 4 * (2 * WIDE - G_SLOTS)], BF16, name="arena", align_bytes=64)
+        narrow = {i: keep.tile([P, 4 * PIECES[i][1]], BF16, name="narrow%d" % i, align_bytes=64) for i in (0, LAST)}
+        codes = {i: keep.tile([P, PIECES[i][1]], U32, name="codes%d" % i, align_bytes=64) for i in range(LAST)}
+        scales = [keep.tile([P, n], U8, name="scales%d" % i, align_bytes=64) for i, (s0, n, sh) in enumerate(PIECES)]
 
-        def gather(i, u):
-            s0, n = SLOT_PIECES[i]
-            if i not in halves:
-                halves.setdefault(i, ring.tile([P, 2, n], U32, name="halves", align_bytes=64))
-            window = hp[u][:].rearrange("p t e -> p (t e)").bitcast(U32)
-            nc.vector.tensor_copy(halves[i][:, u, :], window.indirect(offs_sb[:, s0 // 16 : (s0 + n) // 16]))
+        def rows4(i):
+            if i in narrow:
+                return narrow[i][:]
+            first = 4 * (WIDE - G_SLOTS) * (i % 2)
+            return arena[:, first : first + 4 * WIDE]
 
-        def gather_on_scalar(i, e):
-            s0, n = SLOT_PIECES[i]
-            nc.scalar.activation(
-                halves[i][:, 1, :].bitcast(BF16).rearrange("p (s e) -> p s e", e=2)[:, :, e],
-                rows23[:, e, :].indirect(offs_sb[:, s0 // 16 : (s0 + n) // 16]),
-                COPY,
+        def bring(i):
+            s0, n, shared = PIECES[i]
+            halves.setdefault(i, ring.tile([P, 2, n], U32, name="halves", align_bytes=64))
+            for u, count in ((0, n), (1, n - shared)):
+                window = hp[u][:].rearrange("p t e -> p (t e)").bitcast(U32)
+                nc.vector.tensor_copy(halves[i][:, u, 0:count], window.indirect(offs_sb[:, s0 // 16 : (s0 + count) // 16]))
+            for e in range(2 if shared else 0):
+                nc.scalar.activation(
+                    halves[i][:, 1, n - shared : n].bitcast(BF16).rearrange("p (s e) -> p s e", e=2)[:, :, e],
+                    rows23[:, e, :].indirect(offs_sb[:, (s0 + n - shared) // 16 : (s0 + n) // 16]),
+                    COPY,
+                )
+
+        def weave(copy, i, a, n):
+            copy(
+                rows4(i)[:, 4 * a : 4 * (a + n)].bitcast(U32).rearrange("p (s u) -> p s u", u=2),
+                halves[i][:, :, a : a + n].rearrange("p u s -> p s u"),
             )
 
         def interleave(i):
-            nc.scalar.copy(
-                rows4[i][:].bitcast(F32).rearrange("p (s u) -> p s u", u=2),
-                halves[i][:].bitcast(F32).rearrange("p u s -> p s u"),
-            )
+            n = PIECES[i][1]
+            if i in narrow:
+                weave(nc.scalar.copy, i, 0, n)
+            elif i % 2:
+                weave(nc.gpsimd.tensor_copy, i, 0, G_SLOTS)
+                weave(nc.scalar.copy, i, G_SLOTS, n - G_SLOTS)
+            else:
+                weave(nc.gpsimd.tensor_copy, i, n - G_SLOTS, G_SLOTS)
+                weave(nc.scalar.copy, i, 0, n - G_SLOTS)
 
         y_banks = {}
 
         def second_layer(i):
-            s0, n = SLOT_PIECES[i]
-            nc.vector.quantize_mx(out=codes[i][:].bitcast(FP8X4), scales=scales[i][:], in_=rows4[i][:])
-            bank = y_banks.setdefault(i, psum.tile([P, n], F32, name="y_bank%d" % i, tag="bank%d" % BANK_OF_PIECE[i]))
-            width = min(n, C)
-            for a in range(0, n, width):
+            s0, n, shared = PIECES[i]
+            if i not in codes:
+                codes.setdefault(i, ring.tile([P, n], U32, name="halves", align_bytes=64))
+            nc.vector.quantize_mx(out=codes[i][:].bitcast(FP8X4), scales=scales[i][:], in_=rows4(i))
+            for a in range(0, n, C):
                 e = (s0 + a) // C
+                if a == 0 or i == LAST - 1:
+                    y_banks.setdefault(e, psum.tile([P, C if i >= LAST - 1 else n], F32, name="y_bank%d" % e, tag="bank%d" % Y_BANK[e]))
+                    bank, col = y_banks[e], 0
+                else:
+                    bank, col = y_banks[e - 1], a
                 nc.tensor.matmul_mx(
-                    out=bank[:, a : a + width],
+                    out=bank[:, col : col + C],
                     lhsT=w2w[:, e, :].bitcast(FP8X4),
                     lhsT_scale=w2s[:, e, :],
-                    rhs=codes[i][:, a : a + width].bitcast(FP8X4),
-                    rhs_scale=scales[i][:, a : a + width],
+                    rhs=codes[i][:, a : a + C].bitcast(FP8X4),
+                    rhs_scale=scales[i][:, a : a + C],
                     start=True,
                     stop=True,
                 )
 
-        def empty(i):
-            s0, n = SLOT_PIECES[i]
-            if i == 4:
-                nc.vector.tensor_copy(y[:, s0 : s0 + n], y_banks[i][:])
-            else:
-                nc.scalar.copy(y[:, s0 : s0 + n], y_banks[i][:])
+        def empty(e, copy=nc.scalar.copy):
+            n = y_banks[e][:].shape[1]
+            copy(y[:, e * C : e * C + n], y_banks[e][:])
 
-        def bring(i):
-            gather(i, 0)
-            gather(i, 1)
-            interleave(i)
-
-        gather(0, 0)
-        gather(1, 0)
-        gather(5, 0)
-        gather(6, 0)
-        gather(0, 1)
-        gather_on_scalar(5, 0)
+        bring(0)
+        bring(1)
         interleave(0)
-        gather_on_scalar(5, 1)
-        gather(1, 1)
-        interleave(1)
         second_layer(0)
-        empty(0)
-        gather_on_scalar(6, 0)
-        interleave(5)
-        bring(2)
-        second_layer(1)
-        gather_on_scalar(6, 1)
-        empty(1)
-        bring(3)
-        second_layer(5)
-        second_layer(2)
-        interleave(6)
-        empty(5)
-        empty(2)
-        bring(4)
-        second_layer(3)
-        bring(7)
-        second_layer(6)
-        second_layer(4)
-        second_layer(7)
-        for i in (3, 6, 4, 7):
-            empty(i)
+        for i in range(1, LAST):
+            interleave(i)
+            bring(i + 1)
+            empty(PIECES[i - 1][0] // C)
+            second_layer(i)
+        interleave(LAST)
+        second_layer(LAST)
+        empty(7)
+        empty(8, nc.vector.tensor_copy)
+        empty(9)
 
-        TA = 384
-        TB = T - TA
+        BLOCKS = T // P
+        A0, TA = 3 * P, P
+        LATE = ((0, 3 * P), (4 * P, P))
         prod = keep.tile([P, TOP, T], F32, name="prod", align_bytes=64)
-        turned = keep.tile([P, TA // P, P], F32, name="turned", align_bytes=64)
-        res_a = keep.tile([P, TA], F32, name="res_a", align_bytes=64)
-        res_b = keep.tile([P, TB], F32, name="res_b", align_bytes=64)
-        s01 = keep.tile([P, TB], F32, name="s01", align_bytes=64)
-        s012 = keep.tile([P, TB], F32, name="s012", align_bytes=64)
-        sums = [psum.tile([P, P], F32, name="sum%d" % b, tag="bank%d" % ((6 + b) % 8)) for b in range(TA // P)]
-        back = psum.tile([P, TA], F32, name="back", tag="bank1")
+        turned = keep.tile([P, BLOCKS, P], F32, name="turned", align_bytes=64)
+        res = keep.tile([P, T], F32, name="res", align_bytes=64)
+        sums = [psum.tile([P, P], F32, name="sum%d" % b, tag="bank%d" % SUM_BANKS[b]) for b in range(BLOCKS)]
+        back_a = psum.tile([P, TA], F32, name="back_a", tag="bank%d" % BACK_BANKS[0])
+        backs = [psum.tile([P, n], F32, name="back%d" % g, tag="bank%d" % BACK_BANKS[1 + g]) for g, (t0, n) in enumerate(LATE)]
 
         def fetch(r, t0, n):
             nc.vector.tensor_tensor(
@@ -241,41 +236,33 @@ def tile_moe_sup_lin_relu_kernel(
                 MULT,
             )
 
-        for r in range(TOP):
-            fetch(r, 0, TA)
-            for b in range(TA // P):
-                nc.tensor.matmul(
-                    sums[b][:],
-                    lhsT=prod[:, r, P * b : P * (b + 1)],
-                    rhs=ident[:],
-                    start=(r == 0),
-                    stop=(r == TOP - 1),
-                    is_transpose=True,
-                )
-        for b in range(TA // P):
+        def add_turned(r, b, last):
+            nc.tensor.matmul(
+                sums[b][:], lhsT=prod[:, r, P * b : P * (b + 1)], rhs=ident[:], start=(r == 0), stop=last, is_transpose=True
+            )
+
+        def turn_back(b, dst):
             nc.scalar.copy(turned[:, b, :], sums[b][:])
-            nc.tensor.transpose(back[:, P * b : P * (b + 1)], turned[:, b, :], ident[:])
-        nc.scalar.copy(res_a[:], back[:])
-        nc.sync.dma_start(out[:, 0:TA], res_a[:])
+            nc.tensor.transpose(dst, turned[:, b, :], ident[:])
 
-        def add(dst, left, r, t0):
-            a = t0 - TA
-            nc.vector.tensor_tensor(dst[:, a : a + P], left, prod[:, r, t0 : t0 + P], ADD)
-
-        td, tcc = TA, TA + P
-        fetch(0, td, P)
-        fetch(1, td, P)
-        fetch(0, tcc, P)
-        fetch(1, tcc, P)
-        add(s01, prod[:, 0, td : td + P], 1, td)
-        fetch(2, td, P)
-        add(s01, prod[:, 0, tcc : tcc + P], 1, tcc)
-        fetch(2, tcc, P)
-        fetch(3, td, P)
-        add(s012, s01[:, 0:P], 2, td)
-        add(s012, s01[:, P : 2 * P], 2, tcc)
-        add(res_b, s012[:, 0:P], 3, td)
-        nc.sync.dma_start(out[:, td : td + P], res_b[:, 0:P])
-        fetch(3, tcc, P)
-        add(res_b, s012[:, P : 2 * P], 3, tcc)
-        nc.sync.dma_start(out[:, tcc : tcc + P], res_b[:, P : 2 * P])
+        for r in range(2):
+            fetch(r, 0, T)
+            for b in range(BLOCKS):
+                add_turned(r, b, False)
+        fetch(2, 0, A0)
+        fetch(2, A0, T - A0)
+        fetch(3, A0, TA)
+        for b in range(BLOCKS):
+            add_turned(2, b, b != A0 // P)
+        add_turned(3, A0 // P, True)
+        for g, (t0, n) in enumerate(LATE):
+            for b in range(t0 // P, (t0 + n) // P):
+                turn_back(b, backs[g][:, P * b - t0 : P * (b + 1) - t0])
+        turn_back(A0 // P, back_a[:])
+        nc.scalar.copy(res[:, A0 : A0 + TA], back_a[:])
+        for t0, n in LATE:
+            fetch(3, t0, n)
+        for g, (t0, n) in enumerate(LATE):
+            nc.vector.tensor_tensor(res[:, t0 : t0 + n], prod[:, 3, t0 : t0 + n], backs[g][:], ADD)
+        nc.sync.dma_start(out[:, 0:A0], res[:, 0:A0])
+        nc.sync.dma_start(out[:, A0:T], res[:, A0:T])

@@ -24,13 +24,13 @@ COPY = mybir.ActivationFunctionType.Copy
 P = 128
 T_WIN = 704
 TOKEN_CHUNKS = ((0, 256), (256, 256), (512, 128))
-PIECES = ((0, 256, 0), (256, 512, 0), (768, 512, 352), (1280, 512, 352), (1792, 512, 352), (2304, 256, 0))
+PIECES = ((0, 256, 0), (256, 512, 128), (768, 512, 320), (1280, 512, 320), (1792, 512, 320), (2304, 256, 0))
 LAST = len(PIECES) - 1
 WIDE = 512
 G_SLOTS = 320
-Y_BANK = {0: 6, 1: 7, 3: 0, 5: 1, 7: 2, 8: 3, 9: 4}
-SUM_BANKS = (5, 6, 7, 0, 1)
-BACK_BANKS = (2, 3, 4)
+G_SLOTS_END = 256
+SUM_BANKS = (6, 7, 0, 1, 2)
+BACK_BANKS = (5, 3, 4)
 
 
 def tile_moe_sup_lin_relu_kernel(
@@ -129,9 +129,9 @@ def tile_moe_sup_lin_relu_kernel(
                 else:
                     nc.scalar.activation(dst, src, RELU)
 
-        rows23 = keep.tile([P, 2, T], BF16, name="rows23", align_bytes=64)
+        rows01 = keep.tile([P, 2, T], BF16, name="rows01", align_bytes=64)
         for t0, n in TOKEN_CHUNKS:
-            nc.gpsimd.tensor_copy(rows23[:, :, t0 : t0 + n], hp[1][:, t0 : t0 + n, :].rearrange("p t e -> p e t"))
+            nc.gpsimd.tensor_copy(rows01[:, :, t0 : t0 + n], hp[0][:, t0 : t0 + n, :].rearrange("p t e -> p e t"))
 
         halves = {}
         arena = keep.tile([P, 4 * (2 * WIDE - G_SLOTS)], BF16, name="arena", align_bytes=64)
@@ -148,13 +148,16 @@ def tile_moe_sup_lin_relu_kernel(
         def bring(i):
             s0, n, shared = PIECES[i]
             halves.setdefault(i, ring.tile([P, 2, n], U32, name="halves", align_bytes=64))
-            for u, count in ((0, n), (1, n - shared)):
-                window = hp[u][:].rearrange("p t e -> p (t e)").bitcast(U32)
-                nc.vector.tensor_copy(halves[i][:, u, 0:count], window.indirect(offs_sb[:, s0 // 16 : (s0 + count) // 16]))
+            step = n // 2 if i == LAST else n
+            for a in range(0, n, step):
+                for u, count in ((0, step - shared), (1, step)):
+                    window = hp[u][:].rearrange("p t e -> p (t e)").bitcast(U32)
+                    offsets = offs_sb[:, (s0 + a) // 16 : (s0 + a + count) // 16]
+                    nc.vector.tensor_copy(halves[i][:, u, a : a + count], window.indirect(offsets))
             for e in range(2 if shared else 0):
                 nc.scalar.activation(
-                    halves[i][:, 1, n - shared : n].bitcast(BF16).rearrange("p (s e) -> p s e", e=2)[:, :, e],
-                    rows23[:, e, :].indirect(offs_sb[:, (s0 + n - shared) // 16 : (s0 + n) // 16]),
+                    halves[i][:, 0, n - shared : n].bitcast(BF16).rearrange("p (s e) -> p s e", e=2)[:, :, e],
+                    rows01[:, e, :].indirect(offs_sb[:, (s0 + n - shared) // 16 : (s0 + n) // 16]),
                     COPY,
                 )
 
@@ -166,8 +169,14 @@ def tile_moe_sup_lin_relu_kernel(
 
         def interleave(i):
             n = PIECES[i][1]
-            if i in narrow:
+            if i == 0:
                 weave(nc.scalar.copy, i, 0, n)
+            elif i == LAST:
+                for a in (0, n // 2):
+                    weave(nc.scalar.copy, i, a, n // 2)
+            elif i == LAST - 1:
+                weave(nc.gpsimd.tensor_copy, i, n - G_SLOTS_END, G_SLOTS_END)
+                weave(nc.scalar.copy, i, 0, n - G_SLOTS_END)
             elif i % 2:
                 weave(nc.gpsimd.tensor_copy, i, 0, G_SLOTS)
                 weave(nc.scalar.copy, i, G_SLOTS, n - G_SLOTS)
@@ -177,46 +186,54 @@ def tile_moe_sup_lin_relu_kernel(
 
         y_banks = {}
 
-        def second_layer(i):
-            s0, n, shared = PIECES[i]
+        def second_layer(i, a0, n):
+            s0 = PIECES[i][0] + a0
             if i not in codes:
-                codes.setdefault(i, ring.tile([P, n], U32, name="halves", align_bytes=64))
-            nc.vector.quantize_mx(out=codes[i][:].bitcast(FP8X4), scales=scales[i][:], in_=rows4(i))
-            for a in range(0, n, C):
+                codes.setdefault(i, ring.tile([P, PIECES[i][1]], U32, name="halves", align_bytes=64))
+            nc.vector.quantize_mx(
+                out=codes[i][:, a0 : a0 + n].bitcast(FP8X4),
+                scales=scales[i][:, a0 : a0 + n],
+                in_=rows4(i)[:, 4 * a0 : 4 * (a0 + n)],
+            )
+            bank = psum.tile([P, n], F32, name="y_bank%d" % s0, tag="bank%d" % ((6 + len(y_banks)) % 8))
+            y_banks.setdefault(s0, bank)
+            width = min(n, C)
+            for a in range(0, n, width):
                 e = (s0 + a) // C
-                if a == 0 or i == LAST - 1:
-                    y_banks.setdefault(e, psum.tile([P, C if i >= LAST - 1 else n], F32, name="y_bank%d" % e, tag="bank%d" % Y_BANK[e]))
-                    bank, col = y_banks[e], 0
-                else:
-                    bank, col = y_banks[e - 1], a
                 nc.tensor.matmul_mx(
-                    out=bank[:, col : col + C],
+                    out=bank[:, a : a + width],
                     lhsT=w2w[:, e, :].bitcast(FP8X4),
                     lhsT_scale=w2s[:, e, :],
-                    rhs=codes[i][:, a : a + C].bitcast(FP8X4),
-                    rhs_scale=scales[i][:, a : a + C],
+                    rhs=codes[i][:, a0 + a : a0 + a + width].bitcast(FP8X4),
+                    rhs_scale=scales[i][:, a0 + a : a0 + a + width],
                     start=True,
                     stop=True,
                 )
 
-        def empty(e, copy=nc.scalar.copy):
-            n = y_banks[e][:].shape[1]
-            copy(y[:, e * C : e * C + n], y_banks[e][:])
+        def empty(s0, copy):
+            n = y_banks[s0][:].shape[1]
+            copy(y[:, s0 : s0 + n], y_banks[s0][:])
 
         bring(0)
         bring(1)
         interleave(0)
-        second_layer(0)
+        second_layer(0, 0, PIECES[0][1])
         for i in range(1, LAST):
             interleave(i)
             bring(i + 1)
-            empty(PIECES[i - 1][0] // C)
-            second_layer(i)
+            if i < LAST - 1:
+                empty(PIECES[i - 1][0], nc.scalar.copy)
+                second_layer(i, 0, WIDE)
         interleave(LAST)
-        second_layer(LAST)
-        empty(7)
-        empty(8, nc.vector.tensor_copy)
-        empty(9)
+        empty(PIECES[LAST - 2][0], nc.scalar.copy)
+        for i in (LAST - 1, LAST):
+            s0, n, shared = PIECES[i]
+            for a in (0, n // 2):
+                second_layer(i, a, n // 2)
+        for i, copy in ((LAST - 1, nc.vector.tensor_copy), (LAST, nc.scalar.copy)):
+            s0, n, shared = PIECES[i]
+            for a in (0, n // 2):
+                empty(s0 + a, copy)
 
         BLOCKS = T // P
         A0, TA = 3 * P, P

@@ -22,15 +22,27 @@ RELU = mybir.ActivationFunctionType.Relu
 COPY = mybir.ActivationFunctionType.Copy
 
 P = 128
-T_WIN = 704
+BANKS = 8
+T_PADDED = 704
 TOKEN_CHUNKS = ((0, 256), (256, 256), (512, 128))
-PIECES = ((0, 256, 0), (256, 512, 128), (768, 512, 320), (1280, 512, 320), (1792, 512, 320), (2304, 256, 0))
+H_BANKS = 2 * len(TOKEN_CHUNKS)
+
+WIDE = 2 * C
+SCALAR_FIRST, SCALAR_LATER = 192, 320
+PIECES = (
+    ((0, C, 0), (C, WIDE, SCALAR_FIRST))
+    + tuple((s0, WIDE, SCALAR_LATER) for s0 in range(C + WIDE, S - C, WIDE))
+    + ((S - C, C, 0),)
+)
 LAST = len(PIECES) - 1
-WIDE = 512
-G_SLOTS = 320
-G_SLOTS_END = 256
-SUM_BANKS = (6, 7, 0, 1, 2)
-BACK_BANKS = (5, 3, 4)
+GPSIMD_SLOTS, GPSIMD_SLOTS_LAST_WIDE = 320, 224
+
+BLOCKS = T // P
+FULL_BLOCK = 3
+FULL0 = FULL_BLOCK * P
+LATE = ((0, 2 * P), (2 * P, P), (FULL0 + P, P))
+SUM_BANKS = tuple((H_BANKS + b) % BANKS for b in range(BLOCKS))
+FULL_BACK_BANK, LATE_BACK_BANKS = 5, (3, 4)
 
 
 def tile_moe_sup_lin_relu_kernel(
@@ -55,18 +67,14 @@ def tile_moe_sup_lin_relu_kernel(
         w2w = keep.tile([P, E, N], U32, name="w2w", align_bytes=64)
         w2s = keep.tile([P, E, N], U8, name="w2s", align_bytes=64)
         gates = keep.tile([P, TOP, T], F32, name="gates", align_bytes=64)
-        hp = [keep.tile([P, T_WIN, 2], BF16, name="hp%d" % u, align_bytes=64) for u in range(2)]
+        h_pairs = [keep.tile([P, T_PADDED, 2], BF16, name="h_pairs%d" % u, align_bytes=64) for u in range(2)]
         y = keep.tile([P, S], F32, name="y", align_bytes=64)
-        warm_in = keep.tile([P, 1], F32, name="warm_in")
-        warm_out = keep.tile([P, 1], F32, name="warm_out")
 
         nc.vector.memset(w1s_raw[:].bitcast(I32), 0)
         nc.vector.memset(xs[:].bitcast(I32), 0)
-        nc.vector.memset(warm_in[:], 0.0)
         nc.vector.memset(w2s[:].rearrange("p e n -> p (e n)").bitcast(I32), 0)
         for u in range(2):
-            nc.vector.memset(hp[u][:, T:T_WIN, :], 0.0)
-        nc.scalar.activation(warm_out[:], warm_in[:], RELU)
+            nc.vector.memset(h_pairs[u][:, T:T_PADDED, :], 0.0)
         ident = keep.tile([P, P], F32, name="ident", align_bytes=64)
         nc.vector.memset(ident[:], 0.0)
         make_identity(nc, ident[:], nomemset=True)
@@ -88,120 +96,115 @@ def tile_moe_sup_lin_relu_kernel(
                 w2s[32 * q : 32 * q + 4, :, :].bitcast(I32),
                 w2_scales[:, 0, 4 * q : 4 * q + 4, :].rearrange("e r n -> r e n").bitcast(I32),
             )
-        nc.sync.dma_start(
-            w2w[:].bitcast(I32), w2_words[:, 0].rearrange("e p n d -> p e (n d)").bitcast(I32)
-        )
+        nc.sync.dma_start(w2w[:].bitcast(I32), w2_words[:, 0].rearrange("e p n d -> p e (n d)").bitcast(I32))
         for r, pos in enumerate((pos1, pos2, pos3, pos4)):
             nc.sync.dma_start(pos_sb[r][:], pos)
         nc.sync.dma_start(gates[:], gate.rearrange("r p t -> p r t"))
 
         for u in range(2):
-            planes = slice(2 * u, 2 * u + 2)
+            pair = slice(2 * u, 2 * u + 2)
             nc.vector.tensor_copy(
-                w1s[:].rearrange("p (j m) -> p j m", j=4)[:, planes, :],
-                w1s_raw[:].rearrange("p (m j) -> p j m", j=4)[:, planes, :],
+                w1s[:].rearrange("p (d m) -> p d m", d=4)[:, pair, :],
+                w1s_raw[:].rearrange("p (m d) -> p d m", d=4)[:, pair, :],
             )
             nc.vector.tensor_copy(
-                w1w[:].bitcast(U16).rearrange("p (j m) -> p j m", j=4)[:, planes, :],
-                w1w_raw[:].bitcast(U16).rearrange("p (m j) -> p j m", j=4)[:, planes, :],
+                w1w[:].bitcast(U16).rearrange("p (d m) -> p d m", d=4)[:, pair, :],
+                w1w_raw[:].bitcast(U16).rearrange("p (m d) -> p d m", d=4)[:, pair, :],
             )
-        h_banks = {}
         for u in range(2):
             for c, (t0, n) in enumerate(TOKEN_CHUNKS):
-                bank = h_banks.setdefault(
-                    (u, c), psum.tile([P, 2, n], F32, name="h_bank%d%d" % (u, c), tag="bank%d" % (3 * u + c))
-                )
-                for e in range(2):
-                    j = 2 * u + e
+                h_bank = psum.tile([P, 2, n], F32, name="h_bank%d%d" % (u, c), tag="bank%d" % (len(TOKEN_CHUNKS) * u + c))
+                for v in range(2):
+                    d = 2 * u + v
                     nc.tensor.matmul_mx(
-                        out=bank[:, e, :],
-                        lhsT=w1w[:, 2 * P * j : 2 * P * (j + 1)].bitcast(FP4X4),
-                        lhsT_scale=w1s[:, P * j : P * (j + 1)],
+                        out=h_bank[:, v, :],
+                        lhsT=w1w[:, 2 * P * d : 2 * P * (d + 1)].bitcast(FP4X4),
+                        lhsT_scale=w1s[:, P * d : P * (d + 1)],
                         rhs=xw[:, t0 : t0 + n].bitcast(FP8X4),
                         rhs_scale=xs[:, t0 : t0 + n],
                         start=True,
                         stop=True,
                     )
-                src = bank[:].rearrange("p e t -> p t e")
-                dst = hp[u][:, t0 : t0 + n, :]
-                if u == 0 and c != 1:
+                src = h_bank[:].rearrange("p v t -> p t v")
+                dst = h_pairs[u][:, t0 : t0 + n, :]
+                if u == 0 and c % 2 == 0:
                     nc.vector.tensor_scalar(dst, src, 0.0, None, MAX)
                 else:
                     nc.scalar.activation(dst, src, RELU)
 
-        rows01 = keep.tile([P, 2, T], BF16, name="rows01", align_bytes=64)
-        for t0, n in TOKEN_CHUNKS:
-            nc.gpsimd.tensor_copy(rows01[:, :, t0 : t0 + n], hp[0][:, t0 : t0 + n, :].rearrange("p t e -> p e t"))
+        h_rows = keep.tile([P, 2, T], BF16, name="h_rows", align_bytes=64)
+        for v in range(2):
+            nc.gpsimd.tensor_copy(h_rows[:, v, :], h_pairs[0][:, 0:T, v])
 
-        halves = {}
-        arena = keep.tile([P, 4 * (2 * WIDE - G_SLOTS)], BF16, name="arena", align_bytes=64)
-        narrow = {i: keep.tile([P, 4 * PIECES[i][1]], BF16, name="narrow%d" % i, align_bytes=64) for i in (0, LAST)}
+        runs = {}
+        woven_all = keep.tile([P, 4 * (2 * WIDE - GPSIMD_SLOTS)], BF16, name="woven_all", align_bytes=64)
+        woven_last = keep.tile([P, 4 * PIECES[LAST][1]], BF16, name="woven_last", align_bytes=64)
         codes = {i: keep.tile([P, PIECES[i][1]], U32, name="codes%d" % i, align_bytes=64) for i in range(LAST)}
-        scales = [keep.tile([P, n], U8, name="scales%d" % i, align_bytes=64) for i, (s0, n, sh) in enumerate(PIECES)]
+        scales = [keep.tile([P, n], U8, name="scales%d" % i, align_bytes=64) for i, (s0, n, shared) in enumerate(PIECES)]
 
-        def rows4(i):
-            if i in narrow:
-                return narrow[i][:]
-            first = 4 * (WIDE - G_SLOTS) * (i % 2)
-            return arena[:, first : first + 4 * WIDE]
+        def woven(i):
+            if i == LAST:
+                return woven_last[:]
+            first = 4 * (WIDE - GPSIMD_SLOTS) if i == 0 or i % 2 else 0
+            return woven_all[:, first : first + 4 * PIECES[i][1]]
 
-        def bring(i):
+        def gather_on_vector(i):
             s0, n, shared = PIECES[i]
-            halves.setdefault(i, ring.tile([P, 2, n], U32, name="halves", align_bytes=64))
+            runs.setdefault(i, ring.tile([P, 2, n], U32, name="runs", align_bytes=64))
             step = n // 2 if i == LAST else n
             for a in range(0, n, step):
                 for u, count in ((0, step - shared), (1, step)):
-                    window = hp[u][:].rearrange("p t e -> p (t e)").bitcast(U32)
+                    window = h_pairs[u][:].rearrange("p t v -> p (t v)").bitcast(U32)
                     offsets = offs_sb[:, (s0 + a) // 16 : (s0 + a + count) // 16]
-                    nc.vector.tensor_copy(halves[i][:, u, a : a + count], window.indirect(offsets))
-            for e in range(2 if shared else 0):
-                nc.scalar.activation(
-                    halves[i][:, 0, n - shared : n].bitcast(BF16).rearrange("p (s e) -> p s e", e=2)[:, :, e],
-                    rows01[:, e, :].indirect(offs_sb[:, (s0 + n - shared) // 16 : (s0 + n) // 16]),
-                    COPY,
-                )
+                    nc.vector.tensor_copy(runs[i][:, u, a : a + count], window.indirect(offsets))
 
-        def weave(copy, i, a, n):
-            copy(
-                rows4(i)[:, 4 * a : 4 * (a + n)].bitcast(U32).rearrange("p (s u) -> p s u", u=2),
-                halves[i][:, :, a : a + n].rearrange("p u s -> p s u"),
+        def gather_on_scalar(i, v):
+            s0, n, shared = PIECES[i]
+            nc.scalar.activation(
+                runs[i][:, 0, n - shared : n].bitcast(BF16).rearrange("p (s v) -> p s v", v=2)[:, :, v],
+                h_rows[:, v, :].indirect(offs_sb[:, (s0 + n - shared) // 16 : (s0 + n) // 16]),
+                COPY,
             )
 
-        def interleave(i):
+        def weave_slots(copy, i, a, n):
+            copy(
+                woven(i)[:, 4 * a : 4 * (a + n)].bitcast(U32).rearrange("p (s u) -> p s u", u=2),
+                runs[i][:, :, a : a + n].rearrange("p u s -> p s u"),
+            )
+
+        def weave(i):
             n = PIECES[i][1]
             if i == 0:
-                weave(nc.scalar.copy, i, 0, n)
+                weave_slots(nc.scalar.copy, i, 0, n)
             elif i == LAST:
                 for a in (0, n // 2):
-                    weave(nc.scalar.copy, i, a, n // 2)
-            elif i == LAST - 1:
-                weave(nc.gpsimd.tensor_copy, i, n - G_SLOTS_END, G_SLOTS_END)
-                weave(nc.scalar.copy, i, 0, n - G_SLOTS_END)
+                    weave_slots(nc.scalar.copy, i, a, n // 2)
             elif i % 2:
-                weave(nc.gpsimd.tensor_copy, i, 0, G_SLOTS)
-                weave(nc.scalar.copy, i, G_SLOTS, n - G_SLOTS)
+                weave_slots(nc.gpsimd.tensor_copy, i, 0, GPSIMD_SLOTS)
+                weave_slots(nc.scalar.copy, i, GPSIMD_SLOTS, n - GPSIMD_SLOTS)
             else:
-                weave(nc.gpsimd.tensor_copy, i, n - G_SLOTS, G_SLOTS)
-                weave(nc.scalar.copy, i, 0, n - G_SLOTS)
+                share = GPSIMD_SLOTS_LAST_WIDE if i == LAST - 1 else GPSIMD_SLOTS
+                weave_slots(nc.gpsimd.tensor_copy, i, n - share, share)
+                weave_slots(nc.scalar.copy, i, 0, n - share)
 
         y_banks = {}
 
-        def second_layer(i, a0, n):
+        def quantise_and_multiply(i, a0, n):
             s0 = PIECES[i][0] + a0
             if i not in codes:
-                codes.setdefault(i, ring.tile([P, PIECES[i][1]], U32, name="halves", align_bytes=64))
+                codes.setdefault(i, ring.tile([P, PIECES[i][1]], U32, name="runs", align_bytes=64))
             nc.vector.quantize_mx(
                 out=codes[i][:, a0 : a0 + n].bitcast(FP8X4),
                 scales=scales[i][:, a0 : a0 + n],
-                in_=rows4(i)[:, 4 * a0 : 4 * (a0 + n)],
+                in_=woven(i)[:, 4 * a0 : 4 * (a0 + n)],
             )
-            bank = psum.tile([P, n], F32, name="y_bank%d" % s0, tag="bank%d" % ((6 + len(y_banks)) % 8))
-            y_banks.setdefault(s0, bank)
+            y_bank = psum.tile([P, n], F32, name="y_bank%d" % s0, tag="bank%d" % ((H_BANKS + len(y_banks)) % BANKS))
+            y_banks.setdefault(s0, y_bank)
             width = min(n, C)
             for a in range(0, n, width):
                 e = (s0 + a) // C
                 nc.tensor.matmul_mx(
-                    out=bank[:, a : a + width],
+                    out=y_bank[:, a : a + width],
                     lhsT=w2w[:, e, :].bitcast(FP8X4),
                     lhsT_scale=w2s[:, e, :],
                     rhs=codes[i][:, a0 + a : a0 + a + width].bitcast(FP8X4),
@@ -214,36 +217,38 @@ def tile_moe_sup_lin_relu_kernel(
             n = y_banks[s0][:].shape[1]
             copy(y[:, s0 : s0 + n], y_banks[s0][:])
 
-        bring(0)
-        bring(1)
-        interleave(0)
-        second_layer(0, 0, PIECES[0][1])
-        for i in range(1, LAST):
-            interleave(i)
-            bring(i + 1)
-            if i < LAST - 1:
-                empty(PIECES[i - 1][0], nc.scalar.copy)
-                second_layer(i, 0, WIDE)
-        interleave(LAST)
+        gather_on_vector(0)
+        gather_on_vector(1)
+        gather_on_scalar(1, 0)
+        weave(0)
+        gather_on_scalar(1, 1)
+        quantise_and_multiply(0, 0, PIECES[0][1])
+        for i in range(1, LAST - 1):
+            weave(i)
+            gather_on_vector(i + 1)
+            for v in range(2):
+                gather_on_scalar(i + 1, v)
+            empty(PIECES[i - 1][0], nc.scalar.copy)
+            quantise_and_multiply(i, 0, WIDE)
+        weave(LAST - 1)
+        gather_on_vector(LAST)
+        weave(LAST)
         empty(PIECES[LAST - 2][0], nc.scalar.copy)
         for i in (LAST - 1, LAST):
-            s0, n, shared = PIECES[i]
-            for a in (0, n // 2):
-                second_layer(i, a, n // 2)
+            half = PIECES[i][1] // 2
+            for a in (0, half):
+                quantise_and_multiply(i, a, half)
         for i, copy in ((LAST - 1, nc.vector.tensor_copy), (LAST, nc.scalar.copy)):
-            s0, n, shared = PIECES[i]
-            for a in (0, n // 2):
-                empty(s0 + a, copy)
+            for a in (0, PIECES[i][1] // 2):
+                empty(PIECES[i][0] + a, copy)
 
-        BLOCKS = T // P
-        A0, TA = 3 * P, P
-        LATE = ((0, 3 * P), (4 * P, P))
         prod = keep.tile([P, TOP, T], F32, name="prod", align_bytes=64)
         turned = keep.tile([P, BLOCKS, P], F32, name="turned", align_bytes=64)
         res = keep.tile([P, T], F32, name="res", align_bytes=64)
         sums = [psum.tile([P, P], F32, name="sum%d" % b, tag="bank%d" % SUM_BANKS[b]) for b in range(BLOCKS)]
-        back_a = psum.tile([P, TA], F32, name="back_a", tag="bank%d" % BACK_BANKS[0])
-        backs = [psum.tile([P, n], F32, name="back%d" % g, tag="bank%d" % BACK_BANKS[1 + g]) for g, (t0, n) in enumerate(LATE)]
+        full_back = psum.tile([P, P], F32, name="full_back", tag="bank%d" % FULL_BACK_BANK)
+        late_banks = [psum.tile([P, 2 * P], F32, name="late_bank%d" % k, tag="bank%d" % k) for k in LATE_BACK_BANKS]
+        late_back = [late_banks[0][:], late_banks[1][:, 0:P], late_banks[1][:, P : 2 * P]]
 
         def fetch(r, t0, n):
             nc.vector.tensor_tensor(
@@ -262,24 +267,31 @@ def tile_moe_sup_lin_relu_kernel(
             nc.scalar.copy(turned[:, b, :], sums[b][:])
             nc.tensor.transpose(dst, turned[:, b, :], ident[:])
 
-        for r in range(2):
+        for r in range(TOP - 2):
             fetch(r, 0, T)
             for b in range(BLOCKS):
                 add_turned(r, b, False)
-        fetch(2, 0, A0)
-        fetch(2, A0, T - A0)
-        fetch(3, A0, TA)
+        fetch(TOP - 2, 0, FULL0)
+        fetch(TOP - 2, FULL0, T - FULL0)
+        fetch(TOP - 1, FULL0, P)
         for b in range(BLOCKS):
-            add_turned(2, b, b != A0 // P)
-        add_turned(3, A0 // P, True)
+            add_turned(TOP - 2, b, b != FULL_BLOCK)
+        add_turned(TOP - 1, FULL_BLOCK, True)
         for g, (t0, n) in enumerate(LATE):
-            for b in range(t0 // P, (t0 + n) // P):
-                turn_back(b, backs[g][:, P * b - t0 : P * (b + 1) - t0])
-        turn_back(A0 // P, back_a[:])
-        nc.scalar.copy(res[:, A0 : A0 + TA], back_a[:])
-        for t0, n in LATE:
-            fetch(3, t0, n)
-        for g, (t0, n) in enumerate(LATE):
-            nc.vector.tensor_tensor(res[:, t0 : t0 + n], prod[:, 3, t0 : t0 + n], backs[g][:], ADD)
-        nc.sync.dma_start(out[:, 0:A0], res[:, 0:A0])
-        nc.sync.dma_start(out[:, A0:T], res[:, A0:T])
+            for a in range(0, n, P):
+                turn_back((t0 + a) // P, late_back[g][:, a : a + P])
+        turn_back(FULL_BLOCK, full_back[:])
+        nc.scalar.copy(res[:, FULL0 : FULL0 + P], full_back[:])
+
+        def finish(g):
+            t0, n = LATE[g]
+            nc.vector.tensor_tensor(res[:, t0 : t0 + n], prod[:, TOP - 1, t0 : t0 + n], late_back[g], ADD)
+            first = FULL0 if g == len(LATE) - 1 else t0
+            nc.sync.dma_start(out[:, first : t0 + n], res[:, first : t0 + n])
+
+        fetch(TOP - 1, *LATE[0])
+        fetch(TOP - 1, *LATE[1])
+        finish(0)
+        fetch(TOP - 1, *LATE[2])
+        finish(1)
+        finish(2)

@@ -28,14 +28,14 @@ TOKEN_CHUNKS = ((0, 256), (256, 256), (512, 128))
 H_BANKS = 2 * len(TOKEN_CHUNKS)
 
 WIDE = 2 * C
-SCALAR_FIRST, SCALAR_LATER = 192, 320
+SCALAR_FIRST, SCALAR_LATER = 320, 352
 PIECES = (
     ((0, C, 0), (C, WIDE, SCALAR_FIRST))
     + tuple((s0, WIDE, SCALAR_LATER) for s0 in range(C + WIDE, S - C, WIDE))
     + ((S - C, C, 0),)
 )
 LAST = len(PIECES) - 1
-GPSIMD_SLOTS, GPSIMD_SLOTS_LAST_WIDE = 320, 224
+GPSIMD_SLOTS, GPSIMD_SLOTS_LAST_WIDE = 416, 224
 
 BLOCKS = T // P
 FULL_BLOCK = 3
@@ -175,7 +175,7 @@ def tile_moe_sup_lin_relu_kernel(
         def weave(i):
             n = PIECES[i][1]
             if i == 0:
-                weave_slots(nc.scalar.copy, i, 0, n)
+                weave_slots(nc.gpsimd.tensor_copy, i, 0, n)
             elif i == LAST:
                 for a in (0, n // 2):
                     weave_slots(nc.scalar.copy, i, a, n // 2)

@@ -28,21 +28,19 @@ TOKEN_CHUNKS = ((0, 256), (256, 256), (512, 128))
 H_BANKS = 2 * len(TOKEN_CHUNKS)
 
 WIDE = 2 * C
-SCALAR_FIRST, SCALAR_LATER = 320, 352
+SCALAR_FIRST, SCALAR_SECOND, SCALAR_LATER = 160, 416, 384
 PIECES = (
-    ((0, C, 0), (C, WIDE, SCALAR_FIRST))
-    + tuple((s0, WIDE, SCALAR_LATER) for s0 in range(C + WIDE, S - C, WIDE))
+    ((0, C, 0), (C, WIDE, SCALAR_FIRST), (C + WIDE, WIDE, SCALAR_SECOND))
+    + tuple((s0, WIDE, SCALAR_LATER) for s0 in range(C + 2 * WIDE, S - C, WIDE))
     + ((S - C, C, 0),)
 )
 LAST = len(PIECES) - 1
-GPSIMD_SLOTS, GPSIMD_SLOTS_LAST_WIDE = 416, 224
+GPSIMD_SLOTS, GPSIMD_SLOTS_LAST_WIDE = 416, 256
 
 BLOCKS = T // P
-FULL_BLOCK = 3
-FULL0 = FULL_BLOCK * P
-LATE = ((0, 2 * P), (2 * P, P), (FULL0 + P, P))
+GROUPS = ((0, 3 * P), (3 * P, P), (4 * P, P))
 SUM_BANKS = tuple((H_BANKS + b) % BANKS for b in range(BLOCKS))
-FULL_BACK_BANK, LATE_BACK_BANKS = 5, (3, 4)
+BACK_BANKS = (3, 4, 5)
 
 
 def tile_moe_sup_lin_relu_kernel(
@@ -52,7 +50,7 @@ def tile_moe_sup_lin_relu_kernel(
     with ExitStack() as ctx:
         lists = ctx.enter_context(tc.tile_pool(name="lists", bufs=1))
         keep = ctx.enter_context(tc.tile_pool(name="keep", bufs=1))
-        ring = ctx.enter_context(tc.tile_pool(name="ring", bufs=2))
+        ring = ctx.enter_context(tc.tile_pool(name="ring", bufs=1))
         psum = ctx.enter_context(tc.psum_pool(name="psum", bufs=1))
 
         offs_sb = lists.tile([P, S // 16], U16, name="offs_sb")
@@ -136,7 +134,14 @@ def tile_moe_sup_lin_relu_kernel(
         for v in range(2):
             nc.gpsimd.tensor_copy(h_rows[:, v, :], h_pairs[0][:, 0:T, v])
 
-        runs = {}
+        def new_runs(i):
+            return ring.tile([P, 2, PIECES[i][1]], U32, name="runs%d" % i, tag="runs%d" % (i % 2), align_bytes=64)[:]
+
+        runs = {2: new_runs(2)}
+        runs.setdefault(
+            0,
+            runs[2].rearrange("p u s -> p (u s)")[:, SCALAR_SECOND : SCALAR_SECOND + 2 * C].rearrange("p (u s) -> p u s", u=2),
+        )
         woven_all = keep.tile([P, 4 * (2 * WIDE - GPSIMD_SLOTS)], BF16, name="woven_all", align_bytes=64)
         woven_last = keep.tile([P, 4 * PIECES[LAST][1]], BF16, name="woven_last", align_bytes=64)
         codes = {i: keep.tile([P, PIECES[i][1]], U32, name="codes%d" % i, align_bytes=64) for i in range(LAST)}
@@ -150,19 +155,20 @@ def tile_moe_sup_lin_relu_kernel(
 
         def gather_on_vector(i):
             s0, n, shared = PIECES[i]
-            runs.setdefault(i, ring.tile([P, 2, n], U32, name="runs", align_bytes=64))
+            if i not in runs:
+                runs.setdefault(i, new_runs(i))
             step = n // 2 if i == LAST else n
             for a in range(0, n, step):
-                for u, count in ((0, step - shared), (1, step)):
+                for u, first in ((0, a + shared), (1, a)):
                     window = h_pairs[u][:].rearrange("p t v -> p (t v)").bitcast(U32)
-                    offsets = offs_sb[:, (s0 + a) // 16 : (s0 + a + count) // 16]
-                    nc.vector.tensor_copy(runs[i][:, u, a : a + count], window.indirect(offsets))
+                    offsets = offs_sb[:, (s0 + first) // 16 : (s0 + a + step) // 16]
+                    nc.vector.tensor_copy(runs[i][:, u, first : a + step], window.indirect(offsets))
 
         def gather_on_scalar(i, v):
             s0, n, shared = PIECES[i]
             nc.scalar.activation(
-                runs[i][:, 0, n - shared : n].bitcast(BF16).rearrange("p (s v) -> p s v", v=2)[:, :, v],
-                h_rows[:, v, :].indirect(offs_sb[:, (s0 + n - shared) // 16 : (s0 + n) // 16]),
+                runs[i][:, 0, 0:shared].bitcast(BF16).rearrange("p (s v) -> p s v", v=2)[:, :, v],
+                h_rows[:, v, :].indirect(offs_sb[:, s0 // 16 : (s0 + shared) // 16]),
                 COPY,
             )
 
@@ -192,7 +198,7 @@ def tile_moe_sup_lin_relu_kernel(
         def quantise_and_multiply(i, a0, n):
             s0 = PIECES[i][0] + a0
             if i not in codes:
-                codes.setdefault(i, ring.tile([P, PIECES[i][1]], U32, name="runs", align_bytes=64))
+                codes.setdefault(i, ring.tile([P, PIECES[i][1]], U32, name="codes_last", tag="runs%d" % ((LAST - 1) % 2), align_bytes=64))
             nc.vector.quantize_mx(
                 out=codes[i][:, a0 : a0 + n].bitcast(FP8X4),
                 scales=scales[i][:, a0 : a0 + n],
@@ -222,17 +228,20 @@ def tile_moe_sup_lin_relu_kernel(
         gather_on_scalar(1, 0)
         weave(0)
         gather_on_scalar(1, 1)
+        gather_on_scalar(2, 0)
         quantise_and_multiply(0, 0, PIECES[0][1])
         for i in range(1, LAST - 1):
             weave(i)
             gather_on_vector(i + 1)
-            for v in range(2):
+            for v in range(1 if i == 1 else 0, 2):
                 gather_on_scalar(i + 1, v)
-            empty(PIECES[i - 1][0], nc.scalar.copy)
+            if i < LAST - 2:
+                empty(PIECES[i - 1][0], nc.scalar.copy)
             quantise_and_multiply(i, 0, WIDE)
         weave(LAST - 1)
         gather_on_vector(LAST)
         weave(LAST)
+        empty(PIECES[LAST - 3][0], nc.scalar.copy)
         empty(PIECES[LAST - 2][0], nc.scalar.copy)
         for i in (LAST - 1, LAST):
             half = PIECES[i][1] // 2
@@ -246,9 +255,7 @@ def tile_moe_sup_lin_relu_kernel(
         turned = keep.tile([P, BLOCKS, P], F32, name="turned", align_bytes=64)
         res = keep.tile([P, T], F32, name="res", align_bytes=64)
         sums = [psum.tile([P, P], F32, name="sum%d" % b, tag="bank%d" % SUM_BANKS[b]) for b in range(BLOCKS)]
-        full_back = psum.tile([P, P], F32, name="full_back", tag="bank%d" % FULL_BACK_BANK)
-        late_banks = [psum.tile([P, 2 * P], F32, name="late_bank%d" % k, tag="bank%d" % k) for k in LATE_BACK_BANKS]
-        late_back = [late_banks[0][:], late_banks[1][:, 0:P], late_banks[1][:, P : 2 * P]]
+        back = [psum.tile([P, n], F32, name="back%d" % g, tag="bank%d" % BACK_BANKS[g]) for g, (t0, n) in enumerate(GROUPS)]
 
         def fetch(r, t0, n):
             nc.vector.tensor_tensor(
@@ -258,40 +265,38 @@ def tile_moe_sup_lin_relu_kernel(
                 MULT,
             )
 
-        def add_turned(r, b, last):
+        def add_turned(r, b):
             nc.tensor.matmul(
-                sums[b][:], lhsT=prod[:, r, P * b : P * (b + 1)], rhs=ident[:], start=(r == 0), stop=last, is_transpose=True
+                sums[b][:],
+                lhsT=prod[:, r, P * b : P * (b + 1)],
+                rhs=ident[:],
+                start=(r == 0),
+                stop=(r == TOP - 2),
+                is_transpose=True,
             )
-
-        def turn_back(b, dst):
-            nc.scalar.copy(turned[:, b, :], sums[b][:])
-            nc.tensor.transpose(dst, turned[:, b, :], ident[:])
 
         for r in range(TOP - 2):
             fetch(r, 0, T)
             for b in range(BLOCKS):
-                add_turned(r, b, False)
-        fetch(TOP - 2, 0, FULL0)
-        fetch(TOP - 2, FULL0, T - FULL0)
-        fetch(TOP - 1, FULL0, P)
+                add_turned(r, b)
+        fetch(TOP - 2, *GROUPS[0])
+        fetch(TOP - 2, GROUPS[1][0], T - GROUPS[1][0])
         for b in range(BLOCKS):
-            add_turned(TOP - 2, b, b != FULL_BLOCK)
-        add_turned(TOP - 1, FULL_BLOCK, True)
-        for g, (t0, n) in enumerate(LATE):
+            add_turned(TOP - 2, b)
+        for g, (t0, n) in enumerate(GROUPS):
             for a in range(0, n, P):
-                turn_back((t0 + a) // P, late_back[g][:, a : a + P])
-        turn_back(FULL_BLOCK, full_back[:])
-        nc.scalar.copy(res[:, FULL0 : FULL0 + P], full_back[:])
+                b = (t0 + a) // P
+                nc.scalar.copy(turned[:, b, :], sums[b][:])
+                nc.tensor.transpose(back[g][:, a : a + P], turned[:, b, :], ident[:])
 
         def finish(g):
-            t0, n = LATE[g]
-            nc.vector.tensor_tensor(res[:, t0 : t0 + n], prod[:, TOP - 1, t0 : t0 + n], late_back[g], ADD)
-            first = FULL0 if g == len(LATE) - 1 else t0
-            nc.sync.dma_start(out[:, first : t0 + n], res[:, first : t0 + n])
+            t0, n = GROUPS[g]
+            nc.vector.tensor_tensor(res[:, t0 : t0 + n], prod[:, TOP - 1, t0 : t0 + n], back[g][:], ADD)
+            nc.sync.dma_start(out[:, t0 : t0 + n], res[:, t0 : t0 + n])
 
-        fetch(TOP - 1, *LATE[0])
-        fetch(TOP - 1, *LATE[1])
+        fetch(TOP - 1, *GROUPS[0])
+        fetch(TOP - 1, *GROUPS[1])
         finish(0)
-        fetch(TOP - 1, *LATE[2])
+        fetch(TOP - 1, *GROUPS[2])
         finish(1)
         finish(2)

@@ -69,10 +69,6 @@ def tile_moe_sup_lin_relu_kernel(
         y = keep.tile([P, S], F32, name="y", align_bytes=64)
 
         nc.vector.memset(w1s_raw[:].bitcast(I32), 0)
-        nc.vector.memset(xs[:].bitcast(I32), 0)
-        nc.vector.memset(w2s[:].rearrange("p e n -> p (e n)").bitcast(I32), 0)
-        for u in range(2):
-            nc.vector.memset(h_pairs[u][:, T:T_PADDED, :], 0.0)
         ident = keep.tile([P, P], F32, name="ident", align_bytes=64)
         nc.vector.memset(ident[:], 0.0)
         make_identity(nc, ident[:], nomemset=True)
@@ -80,11 +76,11 @@ def tile_moe_sup_lin_relu_kernel(
         def load_scale_rows(dst, src, q):
             nc.sync.dma_start(dst[32 * q : 32 * q + 4, :].bitcast(I32), src[4 * q : 4 * q + 4, :].bitcast(I32))
 
+        for q in range(2):
+            load_scale_rows(xs, x_scales[0], q)
         nc.sync.dma_start(w1w_raw[:].bitcast(I32), w1_words[0].bitcast(I32))
         for q in range(4):
             load_scale_rows(w1s_raw, w1_scales[0], q)
-        for q in range(2):
-            load_scale_rows(xs, x_scales[0], q)
         nc.sync.dma_start(xw[:].bitcast(I32), x_words[0].rearrange("p t d -> p (t d)").bitcast(I32))
         for q in range(2, 4):
             load_scale_rows(xs, x_scales[0], q)
@@ -275,14 +271,15 @@ def tile_moe_sup_lin_relu_kernel(
                 is_transpose=True,
             )
 
-        for r in range(TOP - 2):
-            fetch(r, 0, T)
-            for b in range(BLOCKS):
-                add_turned(r, b)
-        fetch(TOP - 2, *GROUPS[0])
-        fetch(TOP - 2, GROUPS[1][0], T - GROUPS[1][0])
+        fetch(0, 0, T)
         for b in range(BLOCKS):
-            add_turned(TOP - 2, b)
+            add_turned(0, b)
+        split = GROUPS[1][0]
+        for t0, n in ((0, split), (split, T - split)):
+            for r in range(1, TOP - 1):
+                fetch(r, t0, n)
+                for b in range(t0 // P, (t0 + n) // P):
+                    add_turned(r, b)
         for g, (t0, n) in enumerate(GROUPS):
             for a in range(0, n, P):
                 b = (t0 + a) // P

@@ -28,14 +28,14 @@ TOKEN_CHUNKS = ((0, 256), (256, 256), (512, 128))
 H_BANKS = 2 * len(TOKEN_CHUNKS)
 
 WIDE = 2 * C
-SCALAR_FIRST, SCALAR_SECOND, SCALAR_LATER = 160, 416, 384
+SCALAR_FIRST, SCALAR_SECOND, SCALAR_LATER = 160, 384, 384
 PIECES = (
     ((0, C, 0), (C, WIDE, SCALAR_FIRST), (C + WIDE, WIDE, SCALAR_SECOND))
     + tuple((s0, WIDE, SCALAR_LATER) for s0 in range(C + 2 * WIDE, S - C, WIDE))
     + ((S - C, C, 0),)
 )
 LAST = len(PIECES) - 1
-GPSIMD_SLOTS, GPSIMD_SLOTS_LAST_WIDE = 416, 256
+GPSIMD_SLOTS_LAST_WIDE = 320
 
 BLOCKS = T // P
 GROUPS = ((0, 3 * P), (3 * P, P), (4 * P, P))
@@ -127,8 +127,8 @@ def tile_moe_sup_lin_relu_kernel(
                     nc.scalar.activation(dst, src, RELU)
 
         h_rows = keep.tile([P, 2, T], BF16, name="h_rows", align_bytes=64)
-        for v in range(2):
-            nc.gpsimd.tensor_copy(h_rows[:, v, :], h_pairs[0][:, 0:T, v])
+        for t0, n in TOKEN_CHUNKS:
+            nc.gpsimd.tensor_copy(h_rows[:, :, t0 : t0 + n], h_pairs[0][:, t0 : t0 + n, :].rearrange("p t v -> p v t"))
 
         def new_runs(i):
             return ring.tile([P, 2, PIECES[i][1]], U32, name="runs%d" % i, tag="runs%d" % (i % 2), align_bytes=64)[:]
@@ -138,7 +138,7 @@ def tile_moe_sup_lin_relu_kernel(
             0,
             runs[2].rearrange("p u s -> p (u s)")[:, SCALAR_SECOND : SCALAR_SECOND + 2 * C].rearrange("p (u s) -> p u s", u=2),
         )
-        woven_all = keep.tile([P, 4 * (2 * WIDE - GPSIMD_SLOTS)], BF16, name="woven_all", align_bytes=64)
+        woven_all = keep.tile([P, 4 * 3 * C], BF16, name="woven_all", align_bytes=64)
         woven_last = keep.tile([P, 4 * PIECES[LAST][1]], BF16, name="woven_last", align_bytes=64)
         codes = {i: keep.tile([P, PIECES[i][1]], U32, name="codes%d" % i, align_bytes=64) for i in range(LAST)}
         scales = [keep.tile([P, n], U8, name="scales%d" % i, align_bytes=64) for i, (s0, n, shared) in enumerate(PIECES)]
@@ -146,7 +146,7 @@ def tile_moe_sup_lin_relu_kernel(
         def woven(i):
             if i == LAST:
                 return woven_last[:]
-            first = 4 * (WIDE - GPSIMD_SLOTS) if i == 0 or i % 2 else 0
+            first = 4 * C if i == 0 or i % 2 else 0
             return woven_all[:, first : first + 4 * PIECES[i][1]]
 
         def gather_on_vector(i):
@@ -156,15 +156,18 @@ def tile_moe_sup_lin_relu_kernel(
             step = n // 2 if i == LAST else n
             for a in range(0, n, step):
                 for u, first in ((0, a + shared), (1, a)):
+                    if i == LAST and u == 0 and a > 0:
+                        continue
                     window = h_pairs[u][:].rearrange("p t v -> p (t v)").bitcast(U32)
                     offsets = offs_sb[:, (s0 + first) // 16 : (s0 + a + step) // 16]
                     nc.vector.tensor_copy(runs[i][:, u, first : a + step], window.indirect(offsets))
 
         def gather_on_scalar(i, v):
             s0, n, shared = PIECES[i]
+            a, b = (n // 2, n) if i == LAST else (0, shared)
             nc.scalar.activation(
-                runs[i][:, 0, 0:shared].bitcast(BF16).rearrange("p (s v) -> p s v", v=2)[:, :, v],
-                h_rows[:, v, :].indirect(offs_sb[:, s0 // 16 : (s0 + shared) // 16]),
+                runs[i][:, 0, a:b].bitcast(BF16).rearrange("p (s v) -> p s v", v=2)[:, :, v],
+                h_rows[:, v, :].indirect(offs_sb[:, (s0 + a) // 16 : (s0 + b) // 16]),
                 COPY,
             )
 
@@ -176,23 +179,19 @@ def tile_moe_sup_lin_relu_kernel(
 
         def weave(i):
             n = PIECES[i][1]
-            if i == 0:
+            if i < LAST - 1:
                 weave_slots(nc.gpsimd.tensor_copy, i, 0, n)
             elif i == LAST:
                 for a in (0, n // 2):
                     weave_slots(nc.scalar.copy, i, a, n // 2)
-            elif i % 2:
-                weave_slots(nc.gpsimd.tensor_copy, i, 0, GPSIMD_SLOTS)
-                weave_slots(nc.scalar.copy, i, GPSIMD_SLOTS, n - GPSIMD_SLOTS)
             else:
-                share = GPSIMD_SLOTS_LAST_WIDE if i == LAST - 1 else GPSIMD_SLOTS
+                share = GPSIMD_SLOTS_LAST_WIDE
                 weave_slots(nc.gpsimd.tensor_copy, i, n - share, share)
                 weave_slots(nc.scalar.copy, i, 0, n - share)
 
         y_banks = {}
 
-        def quantise_and_multiply(i, a0, n):
-            s0 = PIECES[i][0] + a0
+        def quantise(i, a0, n):
             if i not in codes:
                 codes.setdefault(i, ring.tile([P, PIECES[i][1]], U32, name="codes_last", tag="runs%d" % ((LAST - 1) % 2), align_bytes=64))
             nc.vector.quantize_mx(
@@ -200,6 +199,9 @@ def tile_moe_sup_lin_relu_kernel(
                 scales=scales[i][:, a0 : a0 + n],
                 in_=woven(i)[:, 4 * a0 : 4 * (a0 + n)],
             )
+
+        def multiply(i, a0, n):
+            s0 = PIECES[i][0] + a0
             y_bank = psum.tile([P, n], F32, name="y_bank%d" % s0, tag="bank%d" % ((H_BANKS + len(y_banks)) % BANKS))
             y_banks.setdefault(s0, y_bank)
             width = min(n, C)
@@ -225,7 +227,8 @@ def tile_moe_sup_lin_relu_kernel(
         weave(0)
         gather_on_scalar(1, 1)
         gather_on_scalar(2, 0)
-        quantise_and_multiply(0, 0, PIECES[0][1])
+        quantise(0, 0, C)
+        multiply(0, 0, C)
         for i in range(1, LAST - 1):
             weave(i)
             gather_on_vector(i + 1)
@@ -233,16 +236,21 @@ def tile_moe_sup_lin_relu_kernel(
                 gather_on_scalar(i + 1, v)
             if i < LAST - 2:
                 empty(PIECES[i - 1][0], nc.scalar.copy)
-            quantise_and_multiply(i, 0, WIDE)
+            for a in (0, C) if i % 2 else (C, 0):
+                quantise(i, a, C)
+            multiply(i, 0, WIDE)
         weave(LAST - 1)
         gather_on_vector(LAST)
+        for v in range(2):
+            gather_on_scalar(LAST, v)
         weave(LAST)
         empty(PIECES[LAST - 3][0], nc.scalar.copy)
         empty(PIECES[LAST - 2][0], nc.scalar.copy)
         for i in (LAST - 1, LAST):
             half = PIECES[i][1] // 2
             for a in (0, half):
-                quantise_and_multiply(i, a, half)
+                quantise(i, a, half)
+                multiply(i, a, half)
         for i, copy in ((LAST - 1, nc.vector.tensor_copy), (LAST, nc.scalar.copy)):
             for a in (0, PIECES[i][1] // 2):
                 empty(PIECES[i][0] + a, copy)

@@ -28,14 +28,14 @@ TOKEN_CHUNKS = ((0, 256), (256, 256), (512, 128))
 H_BANKS = 2 * len(TOKEN_CHUNKS)
 
 WIDE = 2 * C
-SCALAR_FIRST, SCALAR_SECOND, SCALAR_LATER = 160, 384, 384
+SCALAR_FIRST, SCALAR_LATER = 160, 384
 PIECES = (
-    ((0, C, 0), (C, WIDE, SCALAR_FIRST), (C + WIDE, WIDE, SCALAR_SECOND))
-    + tuple((s0, WIDE, SCALAR_LATER) for s0 in range(C + 2 * WIDE, S - C, WIDE))
-    + ((S - C, C, 0),)
+    ((0, C, 0), (C, WIDE, SCALAR_FIRST))
+    + tuple((s0, WIDE, SCALAR_LATER) for s0 in range(C + WIDE, S - C, WIDE))
+    + ((S - C, C, C // 2),)
 )
 LAST = len(PIECES) - 1
-GPSIMD_SLOTS_LAST_WIDE = 320
+GPSIMD_SLOTS_LAST_WIDE = 272
 
 BLOCKS = T // P
 GROUPS = ((0, 3 * P), (3 * P, P), (4 * P, P))
@@ -130,14 +130,14 @@ def tile_moe_sup_lin_relu_kernel(
         for t0, n in TOKEN_CHUNKS:
             nc.gpsimd.tensor_copy(h_rows[:, :, t0 : t0 + n], h_pairs[0][:, t0 : t0 + n, :].rearrange("p t v -> p v t"))
 
-        def new_runs(i):
-            return ring.tile([P, 2, PIECES[i][1]], U32, name="runs%d" % i, tag="runs%d" % (i % 2), align_bytes=64)[:]
-
-        runs = {2: new_runs(2)}
-        runs.setdefault(
-            0,
-            runs[2].rearrange("p u s -> p (u s)")[:, SCALAR_SECOND : SCALAR_SECOND + 2 * C].rearrange("p (u s) -> p u s", u=2),
-        )
+        runs = {}
+        for parity in range(2):
+            first = sum(shared for s0, n, shared in PIECES[parity + 2 :: 2])
+            words = ring.tile([P, first + 2 * WIDE], U32, name="runs%d" % parity, tag="runs%d" % parity, align_bytes=64)
+            for i in range(parity, LAST + 1, 2):
+                if i > parity:
+                    first = first - PIECES[i][2]
+                runs.setdefault(i, words[:, first : first + 2 * PIECES[i][1]].rearrange("p (u s) -> p u s", u=2))
         woven_all = keep.tile([P, 4 * 3 * C], BF16, name="woven_all", align_bytes=64)
         woven_last = keep.tile([P, 4 * PIECES[LAST][1]], BF16, name="woven_last", align_bytes=64)
         codes = {i: keep.tile([P, PIECES[i][1]], U32, name="codes%d" % i, align_bytes=64) for i in range(LAST)}
@@ -146,17 +146,15 @@ def tile_moe_sup_lin_relu_kernel(
         def woven(i):
             if i == LAST:
                 return woven_last[:]
-            first = 4 * C if i == 0 or i % 2 else 0
+            first = 2 * C if i == 0 else 4 * C if i % 2 else 0
             return woven_all[:, first : first + 4 * PIECES[i][1]]
 
         def gather_on_vector(i):
             s0, n, shared = PIECES[i]
-            if i not in runs:
-                runs.setdefault(i, new_runs(i))
             step = n // 2 if i == LAST else n
             for a in range(0, n, step):
-                for u, first in ((0, a + shared), (1, a)):
-                    if i == LAST and u == 0 and a > 0:
+                for u, first in ((0, max(a, shared)), (1, a)):
+                    if first >= a + step:
                         continue
                     window = h_pairs[u][:].rearrange("p t v -> p (t v)").bitcast(U32)
                     offsets = offs_sb[:, (s0 + first) // 16 : (s0 + a + step) // 16]
@@ -164,10 +162,9 @@ def tile_moe_sup_lin_relu_kernel(
 
         def gather_on_scalar(i, v):
             s0, n, shared = PIECES[i]
-            a, b = (n // 2, n) if i == LAST else (0, shared)
             nc.scalar.activation(
-                runs[i][:, 0, a:b].bitcast(BF16).rearrange("p (s v) -> p s v", v=2)[:, :, v],
-                h_rows[:, v, :].indirect(offs_sb[:, (s0 + a) // 16 : (s0 + b) // 16]),
+                runs[i][:, 0, 0:shared].bitcast(BF16).rearrange("p (s v) -> p s v", v=2)[:, :, v],
+                h_rows[:, v, :].indirect(offs_sb[:, s0 // 16 : (s0 + shared) // 16]),
                 COPY,
             )
 
@@ -227,7 +224,8 @@ def tile_moe_sup_lin_relu_kernel(
         weave(0)
         gather_on_scalar(1, 1)
         gather_on_scalar(2, 0)
-        quantise(0, 0, C)
+        for a in (C // 2, 0):
+            quantise(0, a, C // 2)
         multiply(0, 0, C)
         for i in range(1, LAST - 1):
             weave(i)

@@ -35,7 +35,7 @@ PIECES = (
     + ((S - C, C, C // 2),)
 )
 LAST = len(PIECES) - 1
-GPSIMD_SLOTS_LAST_WIDE = 272
+GPSIMD_SLOTS_LAST_WIDE = 256
 
 BLOCKS = T // P
 GROUPS = ((0, 3 * P), (3 * P, P), (4 * P, P))
@@ -140,13 +140,13 @@ def tile_moe_sup_lin_relu_kernel(
                 runs.setdefault(i, words[:, first : first + 2 * PIECES[i][1]].rearrange("p (u s) -> p u s", u=2))
         woven_all = keep.tile([P, 4 * 3 * C], BF16, name="woven_all", align_bytes=64)
         woven_last = keep.tile([P, 4 * PIECES[LAST][1]], BF16, name="woven_last", align_bytes=64)
-        codes = {i: keep.tile([P, PIECES[i][1]], U32, name="codes%d" % i, align_bytes=64) for i in range(LAST)}
+        codes = {i: keep.tile([P, PIECES[i][1]], U32, name="codes%d" % i, align_bytes=64) for i in range(LAST - 1)}
         scales = [keep.tile([P, n], U8, name="scales%d" % i, align_bytes=64) for i, (s0, n, shared) in enumerate(PIECES)]
 
         def woven(i):
             if i == LAST:
                 return woven_last[:]
-            first = 2 * C if i == 0 else 4 * C if i % 2 else 0
+            first = 4 * C if i == 0 or i % 2 else 0
             return woven_all[:, first : first + 4 * PIECES[i][1]]
 
         def gather_on_vector(i):
@@ -190,7 +190,9 @@ def tile_moe_sup_lin_relu_kernel(
 
         def quantise(i, a0, n):
             if i not in codes:
-                codes.setdefault(i, ring.tile([P, PIECES[i][1]], U32, name="codes_last", tag="runs%d" % ((LAST - 1) % 2), align_bytes=64))
+                late = ring.tile([P, WIDE + C], U32, name="codes_late", tag="runs0", align_bytes=64)
+                codes.setdefault(LAST - 1, late[:, 0:WIDE])
+                codes.setdefault(LAST, late[:, WIDE : WIDE + C])
             nc.vector.quantize_mx(
                 out=codes[i][:, a0 : a0 + n].bitcast(FP8X4),
                 scales=scales[i][:, a0 : a0 + n],
@@ -224,8 +226,7 @@ def tile_moe_sup_lin_relu_kernel(
         weave(0)
         gather_on_scalar(1, 1)
         gather_on_scalar(2, 0)
-        for a in (C // 2, 0):
-            quantise(0, a, C // 2)
+        quantise(0, 0, C)
         multiply(0, 0, C)
         for i in range(1, LAST - 1):
             weave(i)

@@ -23,24 +23,17 @@ COPY = mybir.ActivationFunctionType.Copy
 
 P = 128
 BANKS = 8
-T_PADDED = 704
+T_PADDED = 768
+LONG_WINDOW = 1344
 TOKEN_CHUNKS = ((0, 256), (256, 256), (512, 128))
 H_BANKS = 2 * len(TOKEN_CHUNKS)
 
-WIDE = 2 * C
-SCALAR_FIRST, SCALAR_LATER = 160, 384
-PIECES = (
-    ((0, C, 0), (C, WIDE, SCALAR_FIRST))
-    + tuple((s0, WIDE, SCALAR_LATER) for s0 in range(C + WIDE, S - C, WIDE))
-    + ((S - C, C, C // 2),)
-)
+PIECES = ((0, 576, 0), (576, 512, 512), (1088, 480, 288), (1568, 480, 288), (2048, 512, 320))
 LAST = len(PIECES) - 1
-GPSIMD_SLOTS_LAST_WIDE = 256
+QUANTS = ((0, 256), (256, 512), (768, 512), (1280, 512), (1792, 256), (2048, 256), (2304, 128), (2432, 128))
+VECTOR_EMPTIES = (5, 7)
 
-BLOCKS = T // P
-GROUPS = ((0, 3 * P), (3 * P, P), (4 * P, P))
-SUM_BANKS = tuple((H_BANKS + b) % BANKS for b in range(BLOCKS))
-BACK_BANKS = (3, 4, 5)
+FIRST_FREE_BANK = 6
 
 
 def tile_moe_sup_lin_relu_kernel(
@@ -64,8 +57,12 @@ def tile_moe_sup_lin_relu_kernel(
         w1s = keep.tile([P, H], U8, name="w1s", align_bytes=64)
         w2w = keep.tile([P, E, N], U32, name="w2w", align_bytes=64)
         w2s = keep.tile([P, E, N], U8, name="w2s", align_bytes=64)
-        gates = keep.tile([P, TOP, T], F32, name="gates", align_bytes=64)
-        h_pairs = [keep.tile([P, T_PADDED, 2], BF16, name="h_pairs%d" % u, align_bytes=64) for u in range(2)]
+        gates = keep.tile([P, 2, T], F32, name="gates", align_bytes=64)
+        gate_last = keep.tile([P, P], F32, name="gate_last", align_bytes=64)
+        gate_cols = {r: keep.tile([P, 7 - r], F32, name="gate_cols%d" % r, align_bytes=64) for r in (2, 3)}
+        h_all = keep.tile([P, 2 * T_PADDED * 2], BF16, name="h_all", align_bytes=64)
+        h_pairs = [h_all[:, 2 * T_PADDED * u : 2 * T_PADDED * (u + 1)].rearrange("p (t v) -> p t v", v=2) for u in range(2)]
+        h_rows = keep.tile([P, 2, T_PADDED], BF16, name="h_rows", align_bytes=64)
         y = keep.tile([P, S], F32, name="y", align_bytes=64)
 
         nc.vector.memset(w1s_raw[:].bitcast(I32), 0)
@@ -93,7 +90,12 @@ def tile_moe_sup_lin_relu_kernel(
         nc.sync.dma_start(w2w[:].bitcast(I32), w2_words[:, 0].rearrange("e p n d -> p e (n d)").bitcast(I32))
         for r, pos in enumerate((pos1, pos2, pos3, pos4)):
             nc.sync.dma_start(pos_sb[r][:], pos)
-        nc.sync.dma_start(gates[:], gate.rearrange("r p t -> p r t"))
+        nc.sync.dma_start(gates[:], gate[0:2].rearrange("r p t -> p r t"))
+        nc.sync.dma_start(gate_last[:], gate[3, :, T - P : T])
+        with nc.allow_non_contiguous_dma(reason="one gate value for each partition and block of tokens"):
+            for r in (2, 3):
+                blocks = 7 - r
+                nc.sync.dma_start(gate_cols[r][:], gate[r, 0, 0 : blocks * P].rearrange("(b p) -> p b", p=P))
 
         for u in range(2):
             pair = slice(2 * u, 2 * u + 2)
@@ -121,88 +123,68 @@ def tile_moe_sup_lin_relu_kernel(
                     )
                 src = h_bank[:].rearrange("p v t -> p t v")
                 dst = h_pairs[u][:, t0 : t0 + n, :]
-                if u == 0 and c % 2 == 0:
+                if u == 0 and c == 1:
                     nc.vector.tensor_scalar(dst, src, 0.0, None, MAX)
                 else:
                     nc.scalar.activation(dst, src, RELU)
-
-        h_rows = keep.tile([P, 2, T], BF16, name="h_rows", align_bytes=64)
         for t0, n in TOKEN_CHUNKS:
             nc.gpsimd.tensor_copy(h_rows[:, :, t0 : t0 + n], h_pairs[0][:, t0 : t0 + n, :].rearrange("p t v -> p v t"))
 
         runs = {}
-        for parity in range(2):
-            first = sum(shared for s0, n, shared in PIECES[parity + 2 :: 2])
-            words = ring.tile([P, first + 2 * WIDE], U32, name="runs%d" % parity, tag="runs%d" % parity, align_bytes=64)
-            for i in range(parity, LAST + 1, 2):
-                if i > parity:
-                    first = first - PIECES[i][2]
-                runs.setdefault(i, words[:, first : first + 2 * PIECES[i][1]].rearrange("p (u s) -> p u s", u=2))
-        woven_all = keep.tile([P, 4 * 3 * C], BF16, name="woven_all", align_bytes=64)
-        woven_last = keep.tile([P, 4 * PIECES[LAST][1]], BF16, name="woven_last", align_bytes=64)
-        codes = {i: keep.tile([P, PIECES[i][1]], U32, name="codes%d" % i, align_bytes=64) for i in range(LAST - 1)}
-        scales = [keep.tile([P, n], U8, name="scales%d" % i, align_bytes=64) for i, (s0, n, shared) in enumerate(PIECES)]
+        for i, (s0, n, shared) in enumerate(PIECES):
+            tag = "late" if i == LAST - 1 else "runs%d" % i
+            words = ring.tile([P, 2 * n], U32, name="runs%d" % i, tag=tag, align_bytes=64)
+            runs.setdefault(i, words[:].rearrange("p (u s) -> p u s", u=2))
+        woven = keep.tile([P, 4 * S], BF16, name="woven", align_bytes=64)
 
-        def woven(i):
-            if i == LAST:
-                return woven_last[:]
-            first = 4 * C if i == 0 or i % 2 else 0
-            return woven_all[:, first : first + 4 * PIECES[i][1]]
+        def gather_on_vector(i, u, a, b):
+            s0 = PIECES[i][0]
+            columns = LONG_WINDOW if u == 0 and i > 0 else T_PADDED
+            window = h_all[:].bitcast(U32)[:, T_PADDED * u : T_PADDED * u + columns]
+            nc.vector.tensor_copy(runs[i][:, u, a:b], window.indirect(offs_sb[:, (s0 + a) // 16 : (s0 + b) // 16]))
 
-        def gather_on_vector(i):
+        def gather_on_scalar(i):
             s0, n, shared = PIECES[i]
-            step = n // 2 if i == LAST else n
-            for a in range(0, n, step):
-                for u, first in ((0, max(a, shared)), (1, a)):
-                    if first >= a + step:
-                        continue
-                    window = h_pairs[u][:].rearrange("p t v -> p (t v)").bitcast(U32)
-                    offsets = offs_sb[:, (s0 + first) // 16 : (s0 + a + step) // 16]
-                    nc.vector.tensor_copy(runs[i][:, u, first : a + step], window.indirect(offsets))
+            for v in range(2):
+                nc.scalar.activation(
+                    runs[i][:, 0, 0:shared].bitcast(BF16).rearrange("p (s v) -> p s v", v=2)[:, :, v],
+                    h_rows[:, v, :].indirect(offs_sb[:, s0 // 16 : (s0 + shared) // 16]),
+                    COPY,
+                )
 
-        def gather_on_scalar(i, v):
-            s0, n, shared = PIECES[i]
-            nc.scalar.activation(
-                runs[i][:, 0, 0:shared].bitcast(BF16).rearrange("p (s v) -> p s v", v=2)[:, :, v],
-                h_rows[:, v, :].indirect(offs_sb[:, s0 // 16 : (s0 + shared) // 16]),
-                COPY,
-            )
-
-        def weave_slots(copy, i, a, n):
+        def weave(copy, i, a, b):
+            s0 = PIECES[i][0]
             copy(
-                woven(i)[:, 4 * a : 4 * (a + n)].bitcast(U32).rearrange("p (s u) -> p s u", u=2),
-                runs[i][:, :, a : a + n].rearrange("p u s -> p s u"),
+                woven[:, 4 * (s0 + a) : 4 * (s0 + b)].bitcast(U32).rearrange("p (s u) -> p s u", u=2),
+                runs[i][:, :, a:b].rearrange("p u s -> p s u"),
             )
 
-        def weave(i):
-            n = PIECES[i][1]
-            if i < LAST - 1:
-                weave_slots(nc.gpsimd.tensor_copy, i, 0, n)
-            elif i == LAST:
-                for a in (0, n // 2):
-                    weave_slots(nc.scalar.copy, i, a, n // 2)
-            else:
-                share = GPSIMD_SLOTS_LAST_WIDE
-                weave_slots(nc.gpsimd.tensor_copy, i, n - share, share)
-                weave_slots(nc.scalar.copy, i, 0, n - share)
+        gather_on_vector(0, 0, 0, 576)
+        for a, b in ((0, 256), (256, 576)):
+            gather_on_vector(0, 1, a, b)
+            weave(nc.gpsimd.tensor_copy, 0, a, b)
+        for i in range(1, LAST + 1):
+            s0, n, shared = PIECES[i]
+            gather_on_scalar(i)
+            if shared < n:
+                gather_on_vector(i, 0, shared, n)
+            gather_on_vector(i, 1, 0, n)
+            if i < LAST:
+                weave(nc.gpsimd.tensor_copy, i, 0, n)
+        for a in (0, 256):
+            weave(nc.scalar.copy, LAST, a, a + 256)
 
-        y_banks = {}
-
-        def quantise(i, a0, n):
-            if i not in codes:
-                late = ring.tile([P, WIDE + C], U32, name="codes_late", tag="runs0", align_bytes=64)
-                codes.setdefault(LAST - 1, late[:, 0:WIDE])
-                codes.setdefault(LAST, late[:, WIDE : WIDE + C])
+        codes = ring.tile([P, S], U32, name="codes", tag="late", align_bytes=64)
+        scales = keep.tile([P, S], U8, name="scales", align_bytes=64)
+        y_banks = []
+        for j, (s0, n) in enumerate(QUANTS):
             nc.vector.quantize_mx(
-                out=codes[i][:, a0 : a0 + n].bitcast(FP8X4),
-                scales=scales[i][:, a0 : a0 + n],
-                in_=woven(i)[:, 4 * a0 : 4 * (a0 + n)],
+                out=codes[:, s0 : s0 + n].bitcast(FP8X4),
+                scales=scales[:, s0 : s0 + n],
+                in_=woven[:, 4 * s0 : 4 * (s0 + n)],
             )
-
-        def multiply(i, a0, n):
-            s0 = PIECES[i][0] + a0
-            y_bank = psum.tile([P, n], F32, name="y_bank%d" % s0, tag="bank%d" % ((H_BANKS + len(y_banks)) % BANKS))
-            y_banks.setdefault(s0, y_bank)
+            y_bank = psum.tile([P, n], F32, name="y_bank%d" % j, tag="bank%d" % ((H_BANKS + j) % BANKS))
+            y_banks.append(y_bank)
             width = min(n, C)
             for a in range(0, n, width):
                 e = (s0 + a) // C
@@ -210,57 +192,55 @@ def tile_moe_sup_lin_relu_kernel(
                     out=y_bank[:, a : a + width],
                     lhsT=w2w[:, e, :].bitcast(FP8X4),
                     lhsT_scale=w2s[:, e, :],
-                    rhs=codes[i][:, a0 + a : a0 + a + width].bitcast(FP8X4),
-                    rhs_scale=scales[i][:, a0 + a : a0 + a + width],
+                    rhs=codes[:, s0 + a : s0 + a + width].bitcast(FP8X4),
+                    rhs_scale=scales[:, s0 + a : s0 + a + width],
                     start=True,
                     stop=True,
                 )
+            if j not in VECTOR_EMPTIES:
+                nc.scalar.copy(y[:, s0 : s0 + n], y_bank[:])
+        for j in VECTOR_EMPTIES:
+            s0, n = QUANTS[j]
+            nc.vector.tensor_copy(y[:, s0 : s0 + n], y_banks[j][:])
 
-        def empty(s0, copy):
-            n = y_banks[s0][:].shape[1]
-            copy(y[:, s0 : s0 + n], y_banks[s0][:])
-
-        gather_on_vector(0)
-        gather_on_vector(1)
-        gather_on_scalar(1, 0)
-        weave(0)
-        gather_on_scalar(1, 1)
-        gather_on_scalar(2, 0)
-        quantise(0, 0, C)
-        multiply(0, 0, C)
-        for i in range(1, LAST - 1):
-            weave(i)
-            gather_on_vector(i + 1)
-            for v in range(1 if i == 1 else 0, 2):
-                gather_on_scalar(i + 1, v)
-            if i < LAST - 2:
-                empty(PIECES[i - 1][0], nc.scalar.copy)
-            for a in (0, C) if i % 2 else (C, 0):
-                quantise(i, a, C)
-            multiply(i, 0, WIDE)
-        weave(LAST - 1)
-        gather_on_vector(LAST)
-        for v in range(2):
-            gather_on_scalar(LAST, v)
-        weave(LAST)
-        empty(PIECES[LAST - 3][0], nc.scalar.copy)
-        empty(PIECES[LAST - 2][0], nc.scalar.copy)
-        for i in (LAST - 1, LAST):
-            half = PIECES[i][1] // 2
-            for a in (0, half):
-                quantise(i, a, half)
-                multiply(i, a, half)
-        for i, copy in ((LAST - 1, nc.vector.tensor_copy), (LAST, nc.scalar.copy)):
-            for a in (0, PIECES[i][1] // 2):
-                empty(PIECES[i][0] + a, copy)
-
-        prod = keep.tile([P, TOP, T], F32, name="prod", align_bytes=64)
-        turned = keep.tile([P, BLOCKS, P], F32, name="turned", align_bytes=64)
+        prod = keep.tile([P, 2, T], F32, name="prod", align_bytes=64)
+        prod_last = keep.tile([P, P], F32, name="prod_last", align_bytes=64)
+        part = keep.tile([P, T], F32, name="part", align_bytes=64)
+        part_last = keep.tile([P, P], F32, name="part_last", align_bytes=64)
         res = keep.tile([P, T], F32, name="res", align_bytes=64)
-        sums = [psum.tile([P, P], F32, name="sum%d" % b, tag="bank%d" % SUM_BANKS[b]) for b in range(BLOCKS)]
-        back = [psum.tile([P, n], F32, name="back%d" % g, tag="bank%d" % BACK_BANKS[g]) for g, (t0, n) in enumerate(GROUPS)]
+        turned, scaled, back = {}, {}, {}
+        free_banks = ["bank%d" % ((FIRST_FREE_BANK + j) % BANKS) for j in range(BANKS)]
 
-        def fetch(r, t0, n):
+        def fetch_plain(r, t0, n):
+            tile = keep.tile([P, n], F32, name="plain%d_%d" % (r, t0), align_bytes=64)
+            nc.scalar.activation(tile[:], y[:].indirect(pos_sb[r][:, t0 // 16 : (t0 + n) // 16]), COPY)
+            bank_tile = psum.tile([P, n], F32, name="turned%d_%d" % (r, t0), tag=free_banks.pop(0))
+            for a in range(0, n, P):
+                nc.tensor.transpose(bank_tile[:, a : a + P], tile[:, a : a + P], ident[:])
+                turned.setdefault((r, (t0 + a) // P), bank_tile[:, a : a + P])
+
+        def scale(r, b):
+            tile = keep.tile([P, P], F32, name="scaled%d_%d" % (r, b), align_bytes=64)
+            scaled.setdefault((r, b), tile)
+            nc.scalar.activation(tile[:], turned[r, b], COPY, scale=gate_cols[r][:, b : b + 1])
+
+        def turn_back(t0, n):
+            bank_tile = psum.tile([P, n], F32, name="back%d" % t0, tag=free_banks.pop(0))
+            back.setdefault(t0, bank_tile)
+            for a in range(0, n, P):
+                b = (t0 + a) // P
+                rs = [r for r in (2, 3) if (r, b) in scaled]
+                for r in rs:
+                    nc.tensor.matmul(
+                        bank_tile[:, a : a + P],
+                        lhsT=scaled[r, b][:],
+                        rhs=ident[:],
+                        start=(r == rs[0]),
+                        stop=(r == rs[-1]),
+                        is_transpose=True,
+                    )
+
+        def fetch_gated(r, t0, n):
             nc.vector.tensor_tensor(
                 prod[:, r, t0 : t0 + n],
                 y[:].indirect(pos_sb[r][:, t0 // 16 : (t0 + n) // 16]),
@@ -268,39 +248,35 @@ def tile_moe_sup_lin_relu_kernel(
                 MULT,
             )
 
-        def add_turned(r, b):
-            nc.tensor.matmul(
-                sums[b][:],
-                lhsT=prod[:, r, P * b : P * (b + 1)],
-                rhs=ident[:],
-                start=(r == 0),
-                stop=(r == TOP - 2),
-                is_transpose=True,
-            )
+        def add_parts(t0, n):
+            nc.vector.tensor_tensor(part[:, t0 : t0 + n], prod[:, 0, t0 : t0 + n], prod[:, 1, t0 : t0 + n], ADD)
 
-        fetch(0, 0, T)
-        for b in range(BLOCKS):
-            add_turned(0, b)
-        split = GROUPS[1][0]
-        for t0, n in ((0, split), (split, T - split)):
-            for r in range(1, TOP - 1):
-                fetch(r, t0, n)
-                for b in range(t0 // P, (t0 + n) // P):
-                    add_turned(r, b)
-        for g, (t0, n) in enumerate(GROUPS):
-            for a in range(0, n, P):
-                b = (t0 + a) // P
-                nc.scalar.copy(turned[:, b, :], sums[b][:])
-                nc.tensor.transpose(back[g][:, a : a + P], turned[:, b, :], ident[:])
-
-        def finish(g):
-            t0, n = GROUPS[g]
-            nc.vector.tensor_tensor(res[:, t0 : t0 + n], prod[:, TOP - 1, t0 : t0 + n], back[g][:], ADD)
+        def finish(t0, n, sums):
+            nc.vector.tensor_tensor(res[:, t0 : t0 + n], back[t0][:], sums, ADD)
             nc.sync.dma_start(out[:, t0 : t0 + n], res[:, t0 : t0 + n])
 
-        fetch(TOP - 1, *GROUPS[0])
-        fetch(TOP - 1, *GROUPS[1])
-        finish(0)
-        fetch(TOP - 1, *GROUPS[2])
-        finish(1)
-        finish(2)
+        fetch_plain(2, 0, 256)
+        fetch_plain(3, 0, 256)
+        fetch_plain(2, 256, 384)
+        for r in (2, 3):
+            for b in (0, 1):
+                scale(r, b)
+        turn_back(0, 256)
+        fetch_plain(3, 256, 256)
+        for b in (4, 2, 3):
+            scale(2, b)
+        turn_back(512, 128)
+        for b in (2, 3):
+            scale(3, b)
+            turn_back(P * b, P)
+
+        fetch_gated(0, 0, T)
+        fetch_gated(1, 0, T)
+        nc.vector.tensor_tensor(prod_last[:], y[:].indirect(pos_sb[3][:, (T - P) // 16 : T // 16]), gate_last[:], MULT)
+        add_parts(256, 384)
+        add_parts(0, 256)
+        nc.vector.tensor_tensor(part_last[:], prod_last[:], part[:, T - P : T], ADD)
+        finish(0, 256, part[:, 0:256])
+        finish(512, 128, part_last[:])
+        finish(256, 128, part[:, 256:384])
+        finish(384, 128, part[:, 384:512])

@@ -127,8 +127,10 @@ def tile_moe_sup_lin_relu_kernel(
                     nc.vector.tensor_scalar(dst, src, 0.0, None, MAX)
                 else:
                     nc.scalar.activation(dst, src, RELU)
-        for t0, n in TOKEN_CHUNKS:
-            nc.gpsimd.tensor_copy(h_rows[:, :, t0 : t0 + n], h_pairs[0][:, t0 : t0 + n, :].rearrange("p t v -> p v t"))
+        first = TOKEN_CHUNKS[0][1]
+        nc.gpsimd.tensor_copy(h_rows[:, :, 0:first], h_pairs[0][:, 0:first, :].rearrange("p t v -> p v t"))
+        for v in range(2):
+            nc.gpsimd.tensor_copy(h_rows[:, v, first:T], h_pairs[0][:, first:T, v])
 
         runs = {}
         for i, (s0, n, shared) in enumerate(PIECES):

@@ -28,7 +28,7 @@ LONG_WINDOW = 1344
 TOKEN_CHUNKS = ((0, 256), (256, 256), (512, 128))
 H_BANKS = 2 * len(TOKEN_CHUNKS)
 
-PIECES = ((0, 576, 0), (576, 512, 512), (1088, 480, 288), (1568, 480, 288), (2048, 512, 320))
+PIECES = ((0, 576, 0), (576, 512, 512), (1088, 480, 288), (1568, 480, 288), (2048, 512, 256))
 LAST = len(PIECES) - 1
 QUANTS = ((0, 256), (256, 512), (768, 512), (1280, 512), (1792, 256), (2048, 256), (2304, 128), (2432, 128))
 VECTOR_EMPTIES = (5, 7)

@@ -28,8 +28,14 @@ LONG_WINDOW = 1344
 TOKEN_CHUNKS = ((0, 256), (256, 256), (512, 128))
 H_BANKS = 2 * len(TOKEN_CHUNKS)
 
-PIECES = ((0, 576, 0), (576, 512, 512), (1088, 480, 288), (1568, 480, 288), (2048, 512, 256))
-LAST = len(PIECES) - 1
+LATE0, TAIL0 = 1088, 1952
+SCALAR_GATHERS = ((576, 1088), (1088, 1376), (1664, 1952), (1952, 2208))
+VECTOR_GATHERS = (
+    (0, 0, 576), (1, 0, 256), (1, 256, 576), (1, 576, 1088), (0, 1376, 1664), (1, 1088, 1536), (1, 1536, 1952),
+    (1, 1952, 2208), (0, 2208, 2560), (1, 2208, 2560),
+)
+GPSIMD_WEAVES = ((0, 256), (256, 576), (576, 1088), (1088, 1536), (1536, 1952))
+SCALAR_WEAVES = ((1952, 2208), (2208, 2560))
 QUANTS = ((0, 256), (256, 512), (768, 512), (1280, 512), (1792, 256), (2048, 256), (2304, 128), (2432, 128))
 VECTOR_EMPTIES = (5, 7)
 
@@ -132,49 +138,45 @@ def tile_moe_sup_lin_relu_kernel(
         for v in range(2):
             nc.gpsimd.tensor_copy(h_rows[:, v, first:T], h_pairs[0][:, first:T, v])
 
-        runs = {}
-        for i, (s0, n, shared) in enumerate(PIECES):
-            tag = "late" if i == LAST - 1 else "runs%d" % i
-            words = ring.tile([P, 2 * n], U32, name="runs%d" % i, tag=tag, align_bytes=64)
-            runs.setdefault(i, words[:].rearrange("p (u s) -> p u s", u=2))
+        early = keep.tile([P, 2, LATE0], U32, name="early", align_bytes=64)
+        late_words = ring.tile([P, 2 * (TAIL0 - LATE0)], U32, name="late_words", tag="late", align_bytes=64)
+        late = late_words[:].rearrange("p (u s) -> p u s", u=2)
+        tail = keep.tile([P, 2, S - TAIL0], U32, name="tail", align_bytes=64)
         woven = keep.tile([P, 4 * S], BF16, name="woven", align_bytes=64)
 
-        def gather_on_vector(i, u, a, b):
-            s0 = PIECES[i][0]
-            columns = LONG_WINDOW if u == 0 and i > 0 else T_PADDED
-            window = h_all[:].bitcast(U32)[:, T_PADDED * u : T_PADDED * u + columns]
-            nc.vector.tensor_copy(runs[i][:, u, a:b], window.indirect(offs_sb[:, (s0 + a) // 16 : (s0 + b) // 16]))
+        def run(u, a, b):
+            for tile, t0, t1 in ((early, 0, LATE0), (late, LATE0, TAIL0), (tail, TAIL0, S)):
+                if t0 <= a and b <= t1:
+                    return tile[:, u, a - t0 : b - t0]
+            raise ValueError("slots lie in two tiles")
 
-        def gather_on_scalar(i):
-            s0, n, shared = PIECES[i]
+        def gather_on_vector(u, a, b):
+            columns = LONG_WINDOW if u == 0 and a > 0 else T_PADDED
+            window = h_all[:].bitcast(U32)[:, T_PADDED * u : T_PADDED * u + columns]
+            nc.vector.tensor_copy(run(u, a, b), window.indirect(offs_sb[:, a // 16 : b // 16]))
+
+        def gather_on_scalar(a, b):
             for v in range(2):
                 nc.scalar.activation(
-                    runs[i][:, 0, 0:shared].bitcast(BF16).rearrange("p (s v) -> p s v", v=2)[:, :, v],
-                    h_rows[:, v, :].indirect(offs_sb[:, s0 // 16 : (s0 + shared) // 16]),
+                    run(0, a, b).bitcast(BF16).rearrange("p (s v) -> p s v", v=2)[:, :, v],
+                    h_rows[:, v, :].indirect(offs_sb[:, a // 16 : b // 16]),
                     COPY,
                 )
 
-        def weave(copy, i, a, b):
-            s0 = PIECES[i][0]
+        def weave(copy, a, b):
             copy(
-                woven[:, 4 * (s0 + a) : 4 * (s0 + b)].bitcast(U32).rearrange("p (s u) -> p s u", u=2),
-                runs[i][:, :, a:b].rearrange("p u s -> p s u"),
+                woven[:, 4 * a : 4 * b].bitcast(U32).rearrange("p (s u) -> p s u", u=2),
+                run(slice(0, 2), a, b).rearrange("p u s -> p s u"),
             )
 
-        gather_on_vector(0, 0, 0, 576)
-        for a, b in ((0, 256), (256, 576)):
-            gather_on_vector(0, 1, a, b)
-            weave(nc.gpsimd.tensor_copy, 0, a, b)
-        for i in range(1, LAST + 1):
-            s0, n, shared = PIECES[i]
-            gather_on_scalar(i)
-            if shared < n:
-                gather_on_vector(i, 0, shared, n)
-            gather_on_vector(i, 1, 0, n)
-            if i < LAST:
-                weave(nc.gpsimd.tensor_copy, i, 0, n)
-        for a in (0, 256):
-            weave(nc.scalar.copy, LAST, a, a + 256)
+        for a, b in SCALAR_GATHERS:
+            gather_on_scalar(a, b)
+        for u, a, b in VECTOR_GATHERS:
+            gather_on_vector(u, a, b)
+        for a, b in GPSIMD_WEAVES:
+            weave(nc.gpsimd.tensor_copy, a, b)
+        for a, b in SCALAR_WEAVES:
+            weave(nc.scalar.copy, a, b)
 
         codes = ring.tile([P, S], U32, name="codes", tag="late", align_bytes=64)
         scales = keep.tile([P, S], U8, name="scales", align_bytes=64)

@@ -29,13 +29,13 @@ TOKEN_CHUNKS = ((0, 256), (256, 256), (512, 128))
 H_BANKS = 2 * len(TOKEN_CHUNKS)
 
 LATE0, TAIL0 = 1088, 1952
-SCALAR_GATHERS = ((576, 1088), (1088, 1376), (1664, 1952), (1952, 2208))
+SCALAR_GATHERS = ((576, 1088), (1088, 1376), (1664, 1952), (1952, 2368))
 VECTOR_GATHERS = (
     (0, 0, 576), (1, 0, 256), (1, 256, 576), (1, 576, 1088), (0, 1376, 1664), (1, 1088, 1536), (1, 1536, 1952),
-    (1, 1952, 2208), (0, 2208, 2560), (1, 2208, 2560),
+    (1, 1952, 2368), (0, 2368, 2560), (1, 2368, 2560),
 )
 GPSIMD_WEAVES = ((0, 256), (256, 576), (576, 1088), (1088, 1536), (1536, 1952))
-SCALAR_WEAVES = ((1952, 2208), (2208, 2560))
+SCALAR_WEAVES = ((1952, 2368), (2368, 2560))
 QUANTS = ((0, 256), (256, 512), (768, 512), (1280, 512), (1792, 256), (2048, 256), (2304, 128), (2432, 128))
 VECTOR_EMPTIES = (5, 7)
 
@@ -176,7 +176,10 @@ def tile_moe_sup_lin_relu_kernel(
         for a, b in GPSIMD_WEAVES:
             weave(nc.gpsimd.tensor_copy, a, b)
         for a, b in SCALAR_WEAVES:
-            weave(nc.scalar.copy, a, b)
+            nc.scalar.copy(
+                woven[:, 4 * a : 4 * b].rearrange("p (s u v) -> p s u v", u=2, v=2),
+                run(slice(0, 2), a, b).bitcast(BF16).rearrange("p u (s v) -> p s u v", v=2),
+            )
 
         codes = ring.tile([P, S], U32, name="codes", tag="late", align_bytes=64)
         scales = keep.tile([P, S], U8, name="scales", align_bytes=64)

@@ -24,22 +24,22 @@ COPY = mybir.ActivationFunctionType.Copy
 P = 128
 BANKS = 8
 T_PADDED = 768
-LONG_WINDOW = 1344
-TOKEN_CHUNKS = ((0, 256), (256, 256), (512, 128))
-H_BANKS = 2 * len(TOKEN_CHUNKS)
+LONG_WINDOW = 800
+TOKEN_CHUNKS = (((0, 256), (256, 256), (512, 128)), ((128, 256), (384, 256), (0, 128)))
+H_BANKS = 6
 
 LATE0, TAIL0 = 1088, 1952
-SCALAR_GATHERS = ((576, 1088), (1088, 1376), (1664, 1952), (1952, 2368))
+SCALAR_GATHERS = ((576, 1088), (1088, 1408), (1632, 1952), (1952, 2400))
 VECTOR_GATHERS = (
-    (0, 0, 576), (1, 0, 256), (1, 256, 576), (1, 576, 1088), (0, 1376, 1664), (1, 1088, 1536), (1, 1536, 1952),
-    (1, 1952, 2368), (0, 2368, 2560), (1, 2368, 2560),
+    (0, 0, 576), (1, 0, 256), (1, 256, 576), (1, 576, 1088), (0, 1408, 1632), (1, 1088, 1536), (1, 1536, 1952),
+    (1, 1952, 2400), (0, 2400, 2560), (1, 2400, 2560),
 )
 GPSIMD_WEAVES = ((0, 256), (256, 576), (576, 1088), (1088, 1536), (1536, 1952))
-SCALAR_WEAVES = ((1952, 2368), (2368, 2560))
-QUANTS = ((0, 256), (256, 512), (768, 512), (1280, 512), (1792, 256), (2048, 256), (2304, 128), (2432, 128))
-VECTOR_EMPTIES = (5, 7)
+SCALAR_WEAVES = ((1952, 2400), (2400, 2560))
+Y_BANKS = ((0, 512), (512, 512), (1024, 512), (1536, 256), (1792, 256), (2048, 256), (2304, 128), (2432, 64), (2496, 64))
+VECTOR_EMPTIES = (3, 5, 7)
 
-FIRST_FREE_BANK = 6
+FIRST_FREE_BANK = 7
 
 
 def tile_moe_sup_lin_relu_kernel(
@@ -64,8 +64,8 @@ def tile_moe_sup_lin_relu_kernel(
         w2w = keep.tile([P, E, N], U32, name="w2w", align_bytes=64)
         w2s = keep.tile([P, E, N], U8, name="w2s", align_bytes=64)
         gates = keep.tile([P, 2, T], F32, name="gates", align_bytes=64)
-        gate_last = keep.tile([P, P], F32, name="gate_last", align_bytes=64)
-        gate_cols = {r: keep.tile([P, 7 - r], F32, name="gate_cols%d" % r, align_bytes=64) for r in (2, 3)}
+        gate_last = keep.tile([P, 2 * P], F32, name="gate_last", align_bytes=64)
+        gate_cols = {r: keep.tile([P, 9 - 2 * r], F32, name="gate_cols%d" % r, align_bytes=64) for r in (2, 3)}
         h_all = keep.tile([P, 2 * T_PADDED * 2], BF16, name="h_all", align_bytes=64)
         h_pairs = [h_all[:, 2 * T_PADDED * u : 2 * T_PADDED * (u + 1)].rearrange("p (t v) -> p t v", v=2) for u in range(2)]
         h_rows = keep.tile([P, 2, T_PADDED], BF16, name="h_rows", align_bytes=64)
@@ -97,10 +97,10 @@ def tile_moe_sup_lin_relu_kernel(
         for r, pos in enumerate((pos1, pos2, pos3, pos4)):
             nc.sync.dma_start(pos_sb[r][:], pos)
         nc.sync.dma_start(gates[:], gate[0:2].rearrange("r p t -> p r t"))
-        nc.sync.dma_start(gate_last[:], gate[3, :, T - P : T])
+        nc.sync.dma_start(gate_last[:], gate[3, :, T - 2 * P : T])
         with nc.allow_non_contiguous_dma(reason="one gate value for each partition and block of tokens"):
             for r in (2, 3):
-                blocks = 7 - r
+                blocks = 9 - 2 * r
                 nc.sync.dma_start(gate_cols[r][:], gate[r, 0, 0 : blocks * P].rearrange("(b p) -> p b", p=P))
 
         for u in range(2):
@@ -114,8 +114,8 @@ def tile_moe_sup_lin_relu_kernel(
                 w1w_raw[:].bitcast(U16).rearrange("p (m d) -> p d m", d=4)[:, pair, :],
             )
         for u in range(2):
-            for c, (t0, n) in enumerate(TOKEN_CHUNKS):
-                h_bank = psum.tile([P, 2, n], F32, name="h_bank%d%d" % (u, c), tag="bank%d" % (len(TOKEN_CHUNKS) * u + c))
+            for c, (t0, n) in enumerate(TOKEN_CHUNKS[u]):
+                h_bank = psum.tile([P, 2, n], F32, name="h_bank%d%d" % (u, c), tag="bank%d" % (3 * u + c))
                 for v in range(2):
                     d = 2 * u + v
                     nc.tensor.matmul_mx(
@@ -129,11 +129,11 @@ def tile_moe_sup_lin_relu_kernel(
                     )
                 src = h_bank[:].rearrange("p v t -> p t v")
                 dst = h_pairs[u][:, t0 : t0 + n, :]
-                if u == 0 and c == 1:
+                if u == 0 and c < 2:
                     nc.vector.tensor_scalar(dst, src, 0.0, None, MAX)
                 else:
                     nc.scalar.activation(dst, src, RELU)
-        first = TOKEN_CHUNKS[0][1]
+        first = TOKEN_CHUNKS[0][0][1]
         nc.gpsimd.tensor_copy(h_rows[:, :, 0:first], h_pairs[0][:, 0:first, :].rearrange("p t v -> p v t"))
         for v in range(2):
             nc.gpsimd.tensor_copy(h_rows[:, v, first:T], h_pairs[0][:, first:T, v])
@@ -184,36 +184,35 @@ def tile_moe_sup_lin_relu_kernel(
         codes = ring.tile([P, S], U32, name="codes", tag="late", align_bytes=64)
         scales = keep.tile([P, S], U8, name="scales", align_bytes=64)
         y_banks = []
-        for j, (s0, n) in enumerate(QUANTS):
-            nc.vector.quantize_mx(
-                out=codes[:, s0 : s0 + n].bitcast(FP8X4),
-                scales=scales[:, s0 : s0 + n],
-                in_=woven[:, 4 * s0 : 4 * (s0 + n)],
-            )
+        for j, (s0, n) in enumerate(Y_BANKS):
             y_bank = psum.tile([P, n], F32, name="y_bank%d" % j, tag="bank%d" % ((H_BANKS + j) % BANKS))
             y_banks.append(y_bank)
             width = min(n, C)
-            for a in range(0, n, width):
-                e = (s0 + a) // C
+            for a in range(s0, s0 + n, width):
+                nc.vector.quantize_mx(
+                    out=codes[:, a : a + width].bitcast(FP8X4),
+                    scales=scales[:, a : a + width],
+                    in_=woven[:, 4 * a : 4 * (a + width)],
+                )
                 nc.tensor.matmul_mx(
-                    out=y_bank[:, a : a + width],
-                    lhsT=w2w[:, e, :].bitcast(FP8X4),
-                    lhsT_scale=w2s[:, e, :],
-                    rhs=codes[:, s0 + a : s0 + a + width].bitcast(FP8X4),
-                    rhs_scale=scales[:, s0 + a : s0 + a + width],
+                    out=y_bank[:, a - s0 : a - s0 + width],
+                    lhsT=w2w[:, a // C, :].bitcast(FP8X4),
+                    lhsT_scale=w2s[:, a // C, :],
+                    rhs=codes[:, a : a + width].bitcast(FP8X4),
+                    rhs_scale=scales[:, a : a + width],
                     start=True,
                     stop=True,
                 )
             if j not in VECTOR_EMPTIES:
                 nc.scalar.copy(y[:, s0 : s0 + n], y_bank[:])
         for j in VECTOR_EMPTIES:
-            s0, n = QUANTS[j]
+            s0, n = Y_BANKS[j]
             nc.vector.tensor_copy(y[:, s0 : s0 + n], y_banks[j][:])
 
         prod = keep.tile([P, 2, T], F32, name="prod", align_bytes=64)
-        prod_last = keep.tile([P, P], F32, name="prod_last", align_bytes=64)
+        prod_last = keep.tile([P, 2 * P], F32, name="prod_last", align_bytes=64)
         part = keep.tile([P, T], F32, name="part", align_bytes=64)
-        part_last = keep.tile([P, P], F32, name="part_last", align_bytes=64)
+        half_last = keep.tile([P, 2 * P], F32, name="half_last", align_bytes=64)
         res = keep.tile([P, T], F32, name="res", align_bytes=64)
         turned, scaled, back = {}, {}, {}
         free_banks = ["bank%d" % ((FIRST_FREE_BANK + j) % BANKS) for j in range(BANKS)]
@@ -263,27 +262,24 @@ def tile_moe_sup_lin_relu_kernel(
             nc.sync.dma_start(out[:, t0 : t0 + n], res[:, t0 : t0 + n])
 
         fetch_plain(2, 0, 256)
-        fetch_plain(3, 0, 256)
+        fetch_plain(3, 0, 384)
         fetch_plain(2, 256, 384)
         for r in (2, 3):
             for b in (0, 1):
                 scale(r, b)
         turn_back(0, 256)
-        fetch_plain(3, 256, 256)
-        for b in (4, 2, 3):
+        for b in (3, 4):
             scale(2, b)
-        turn_back(512, 128)
-        for b in (2, 3):
-            scale(3, b)
-            turn_back(P * b, P)
+        turn_back(384, 256)
+        for r in (3, 2):
+            scale(r, 2)
+        turn_back(256, 128)
 
+        nc.vector.tensor_tensor(prod_last[:], y[:].indirect(pos_sb[3][:, (T - 2 * P) // 16 : T // 16]), gate_last[:], MULT)
         fetch_gated(0, 0, T)
         fetch_gated(1, 0, T)
-        nc.vector.tensor_tensor(prod_last[:], y[:].indirect(pos_sb[3][:, (T - P) // 16 : T // 16]), gate_last[:], MULT)
-        add_parts(256, 384)
-        add_parts(0, 256)
-        nc.vector.tensor_tensor(part_last[:], prod_last[:], part[:, T - P : T], ADD)
-        finish(0, 256, part[:, 0:256])
-        finish(512, 128, part_last[:])
-        finish(256, 128, part[:, 256:384])
-        finish(384, 128, part[:, 384:512])
+        nc.vector.tensor_tensor(half_last[:], prod_last[:], prod[:, 0, T - 2 * P : T], ADD)
+        add_parts(0, 384)
+        nc.vector.tensor_tensor(part[:, T - 2 * P : T], half_last[:], prod[:, 1, T - 2 * P : T], ADD)
+        for t0, n in ((0, 256), (384, 256), (256, 128)):
+            finish(t0, n, part[:, t0 : t0 + n])

from contextlib import ExitStack

import concourse.mybir as mybir
from concourse.masks import make_identity

K, T, E, C, H, N, TOP = 512, 640, 10, 256, 512, 128, 4
S = E * C
FLOPS = 2 * K * H * T + 2 * H * N * S

F32 = mybir.dt.float32
BF16 = mybir.dt.bfloat16
I32 = mybir.dt.int32
U32 = mybir.dt.uint32
U16 = mybir.dt.uint16
U8 = mybir.dt.uint8
FP8X4 = mybir.dt.float8_e4m3fn_x4
FP4X4 = mybir.dt.float4_e2m1fn_x4
MULT = mybir.AluOpType.mult
ADD = mybir.AluOpType.add
MAX = mybir.AluOpType.max
RELU = mybir.ActivationFunctionType.Relu
COPY = mybir.ActivationFunctionType.Copy

P = 128
BANKS = 8
T_PADDED = 768
LONG_WINDOW = 800
TOKEN_CHUNKS = (((0, 256), (256, 256), (512, 128)), ((128, 256), (384, 256), (0, 128)))
H_BANKS = 6

LATE0, TAIL0 = 1088, 1952
SCALAR_GATHERS = ((576, 1088), (1088, 1408), (1632, 1952), (1952, 2400))
VECTOR_GATHERS = (
    (0, 0, 576), (1, 0, 256), (1, 256, 576), (1, 576, 1088), (0, 1408, 1632), (1, 1088, 1536), (1, 1536, 1952),
    (1, 1952, 2400), (0, 2400, 2560), (1, 2400, 2560),
)
GPSIMD_WEAVES = ((0, 256), (256, 576), (576, 1088), (1088, 1536), (1536, 1952))
SCALAR_WEAVES = ((1952, 2400), (2400, 2560))
Y_BANKS = ((0, 512), (512, 512), (1024, 512), (1536, 256), (1792, 256), (2048, 256), (2304, 128), (2432, 64), (2496, 64))
VECTOR_EMPTIES = (3, 5, 7)

FIRST_FREE_BANK = 7


def tile_moe_sup_lin_relu_kernel(
    tc, x_words, x_scales, w1_words, w1_scales, w2_words, w2_scales, gate, offs, pos1, pos2, pos3, pos4, out
):
    nc = tc.nc
    with ExitStack() as ctx:
        lists = ctx.enter_context(tc.tile_pool(name="lists", bufs=1))
        keep = ctx.enter_context(tc.tile_pool(name="keep", bufs=1))
        ring = ctx.enter_context(tc.tile_pool(name="ring", bufs=1))
        psum = ctx.enter_context(tc.psum_pool(name="psum", bufs=1))

        offs_sb = lists.tile([P, S // 16], U16, name="offs_sb")
        pos_sb = [lists.tile([P, T // 16], U16, name="pos_sb%d" % r) for r in range(TOP)]

        xw = keep.tile([P, T], U32, name="xw", align_bytes=64)
        xs = keep.tile([P, T], U8, name="xs", align_bytes=64)
        w1w_raw = keep.tile([P, 2 * H], U8, name="w1w_raw", align_bytes=64)
        w1s_raw = keep.tile([P, H], U8, name="w1s_raw", align_bytes=64)
        w1w = keep.tile([P, 2 * H], U8, name="w1w", align_bytes=64)
        w1s = keep.tile([P, H], U8, name="w1s", align_bytes=64)
        w2w = keep.tile([P, E, N], U32, name="w2w", align_bytes=64)
        w2s = keep.tile([P, E, N], U8, name="w2s", align_bytes=64)
        gates = keep.tile([P, 2, T], F32, name="gates", align_bytes=64)
        gate_last = keep.tile([P, 2 * P], F32, name="gate_last", align_bytes=64)
        gate_cols = {r: keep.tile([P, 9 - 2 * r], F32, name="gate_cols%d" % r, align_bytes=64) for r in (2, 3)}
        h_all = keep.tile([P, 2 * T_PADDED * 2], BF16, name="h_all", align_bytes=64)
        h_pairs = [h_all[:, 2 * T_PADDED * u : 2 * T_PADDED * (u + 1)].rearrange("p (t v) -> p t v", v=2) for u in range(2)]
        h_rows = keep.tile([P, 2, T_PADDED], BF16, name="h_rows", align_bytes=64)
        y = keep.tile([P, S], F32, name="y", align_bytes=64)

        nc.vector.memset(w1s_raw[:].bitcast(I32), 0)
        ident = keep.tile([P, P], F32, name="ident", align_bytes=64)
        nc.vector.memset(ident[:], 0.0)
        make_identity(nc, ident[:], nomemset=True)

        def load_scale_rows(dst, src, q):
            nc.sync.dma_start(dst[32 * q : 32 * q + 4, :].bitcast(I32), src[4 * q : 4 * q + 4, :].bitcast(I32))

        for q in range(2):
            load_scale_rows(xs, x_scales[0], q)
        nc.sync.dma_start(w1w_raw[:].bitcast(I32), w1_words[0].bitcast(I32))
        for q in range(4):
            load_scale_rows(w1s_raw, w1_scales[0], q)
        nc.sync.dma_start(xw[:].bitcast(I32), x_words[0].rearrange("p t d -> p (t d)").bitcast(I32))
        for q in range(2, 4):
            load_scale_rows(xs, x_scales[0], q)
        nc.sync.dma_start(offs_sb[:], offs)
        for q in range(4):
            nc.sync.dma_start(
                w2s[32 * q : 32 * q + 4, :, :].bitcast(I32),
                w2_scales[:, 0, 4 * q : 4 * q + 4, :].rearrange("e r n -> r e n").bitcast(I32),
            )
        nc.sync.dma_start(w2w[:].bitcast(I32), w2_words[:, 0].rearrange("e p n d -> p e (n d)").bitcast(I32))
        for r, pos in enumerate((pos1, pos2, pos3, pos4)):
            nc.sync.dma_start(pos_sb[r][:], pos)
        nc.sync.dma_start(gates[:], gate[0:2].rearrange("r p t -> p r t"))
        nc.sync.dma_start(gate_last[:], gate[3, :, T - 2 * P : T])
        with nc.allow_non_contiguous_dma(reason="one gate value for each partition and block of tokens"):
            for r in (2, 3):
                blocks = 9 - 2 * r
                nc.sync.dma_start(gate_cols[r][:], gate[r, 0, 0 : blocks * P].rearrange("(b p) -> p b", p=P))

        for u in range(2):
            pair = slice(2 * u, 2 * u + 2)
            nc.vector.tensor_copy(
                w1s[:].rearrange("p (d m) -> p d m", d=4)[:, pair, :],
                w1s_raw[:].rearrange("p (m d) -> p d m", d=4)[:, pair, :],
            )
            nc.vector.tensor_copy(
                w1w[:].bitcast(U16).rearrange("p (d m) -> p d m", d=4)[:, pair, :],
                w1w_raw[:].bitcast(U16).rearrange("p (m d) -> p d m", d=4)[:, pair, :],
            )
        for u in range(2):
            for c, (t0, n) in enumerate(TOKEN_CHUNKS[u]):
                h_bank = psum.tile([P, 2, n], F32, name="h_bank%d%d" % (u, c), tag="bank%d" % (3 * u + c))
                for v in range(2):
                    d = 2 * u + v
                    nc.tensor.matmul_mx(
                        out=h_bank[:, v, :],
                        lhsT=w1w[:, 2 * P * d : 2 * P * (d + 1)].bitcast(FP4X4),
                        lhsT_scale=w1s[:, P * d : P * (d + 1)],
                        rhs=xw[:, t0 : t0 + n].bitcast(FP8X4),
                        rhs_scale=xs[:, t0 : t0 + n],
                        start=True,
                        stop=True,
                    )
                src = h_bank[:].rearrange("p v t -> p t v")
                dst = h_pairs[u][:, t0 : t0 + n, :]
                if u == 0 and c < 2:
                    nc.vector.tensor_scalar(dst, src, 0.0, None, MAX)
                else:
                    nc.scalar.activation(dst, src, RELU)
        first = TOKEN_CHUNKS[0][0][1]
        nc.gpsimd.tensor_copy(h_rows[:, :, 0:first], h_pairs[0][:, 0:first, :].rearrange("p t v -> p v t"))
        for v in range(2):
            nc.gpsimd.tensor_copy(h_rows[:, v, first:T], h_pairs[0][:, first:T, v])

        early = keep.tile([P, 2, LATE0], U32, name="early", align_bytes=64)
        late_words = ring.tile([P, 2 * (TAIL0 - LATE0)], U32, name="late_words", tag="late", align_bytes=64)
        late = late_words[:].rearrange("p (u s) -> p u s", u=2)
        tail = keep.tile([P, 2, S - TAIL0], U32, name="tail", align_bytes=64)
        woven = keep.tile([P, 4 * S], BF16, name="woven", align_bytes=64)

        def run(u, a, b):
            for tile, t0, t1 in ((early, 0, LATE0), (late, LATE0, TAIL0), (tail, TAIL0, S)):
                if t0 <= a and b <= t1:
                    return tile[:, u, a - t0 : b - t0]
            raise ValueError("slots lie in two tiles")

        def gather_on_vector(u, a, b):
            columns = LONG_WINDOW if u == 0 and a > 0 else T_PADDED
            window = h_all[:].bitcast(U32)[:, T_PADDED * u : T_PADDED * u + columns]
            nc.vector.tensor_copy(run(u, a, b), window.indirect(offs_sb[:, a // 16 : b // 16]))

        def gather_on_scalar(a, b):
            for v in range(2):
                nc.scalar.activation(
                    run(0, a, b).bitcast(BF16).rearrange("p (s v) -> p s v", v=2)[:, :, v],
                    h_rows[:, v, :].indirect(offs_sb[:, a // 16 : b // 16]),
                    COPY,
                )

        def weave(copy, a, b):
            copy(
                woven[:, 4 * a : 4 * b].bitcast(U32).rearrange("p (s u) -> p s u", u=2),
                run(slice(0, 2), a, b).rearrange("p u s -> p s u"),
            )

        for a, b in SCALAR_GATHERS:
            gather_on_scalar(a, b)
        for u, a, b in VECTOR_GATHERS:
            gather_on_vector(u, a, b)
        for a, b in GPSIMD_WEAVES:
            weave(nc.gpsimd.tensor_copy, a, b)
        for a, b in SCALAR_WEAVES:
            nc.scalar.copy(
                woven[:, 4 * a : 4 * b].rearrange("p (s u v) -> p s u v", u=2, v=2),
                run(slice(0, 2), a, b).bitcast(BF16).rearrange("p u (s v) -> p s u v", v=2),
            )

        codes = ring.tile([P, S], U32, name="codes", tag="late", align_bytes=64)
        scales = keep.tile([P, S], U8, name="scales", align_bytes=64)
        y_banks = []
        for j, (s0, n) in enumerate(Y_BANKS):
            y_bank = psum.tile([P, n], F32, name="y_bank%d" % j, tag="bank%d" % ((H_BANKS + j) % BANKS))
            y_banks.append(y_bank)
            width = min(n, C)
            for a in range(s0, s0 + n, width):
                nc.vector.quantize_mx(
                    out=codes[:, a : a + width].bitcast(FP8X4),
                    scales=scales[:, a : a + width],
                    in_=woven[:, 4 * a : 4 * (a + width)],
                )
                nc.tensor.matmul_mx(
                    out=y_bank[:, a - s0 : a - s0 + width],
                    lhsT=w2w[:, a // C, :].bitcast(FP8X4),
                    lhsT_scale=w2s[:, a // C, :],
                    rhs=codes[:, a : a + width].bitcast(FP8X4),
                    rhs_scale=scales[:, a : a + width],
                    start=True,
                    stop=True,
                )
            if j not in VECTOR_EMPTIES:
                nc.scalar.copy(y[:, s0 : s0 + n], y_bank[:])
        for j in VECTOR_EMPTIES:
            s0, n = Y_BANKS[j]
            nc.vector.tensor_copy(y[:, s0 : s0 + n], y_banks[j][:])

        prod = keep.tile([P, 2, T], F32, name="prod", align_bytes=64)
        prod_last = keep.tile([P, 2 * P], F32, name="prod_last", align_bytes=64)
        part = keep.tile([P, T], F32, name="part", align_bytes=64)
        half_last = keep.tile([P, 2 * P], F32, name="half_last", align_bytes=64)
        res = keep.tile([P, T], F32, name="res", align_bytes=64)
        turned, scaled, back = {}, {}, {}
        free_banks = ["bank%d" % ((FIRST_FREE_BANK + j) % BANKS) for j in range(BANKS)]

        def fetch_plain(r, t0, n):
            tile = keep.tile([P, n], F32, name="plain%d_%d" % (r, t0), align_bytes=64)
            nc.scalar.activation(tile[:], y[:].indirect(pos_sb[r][:, t0 // 16 : (t0 + n) // 16]), COPY)
            bank_tile = psum.tile([P, n], F32, name="turned%d_%d" % (r, t0), tag=free_banks.pop(0))
            for a in range(0, n, P):
                nc.tensor.transpose(bank_tile[:, a : a + P], tile[:, a : a + P], ident[:])
                turned.setdefault((r, (t0 + a) // P), bank_tile[:, a : a + P])

        def scale(r, b):
            tile = keep.tile([P, P], F32, name="scaled%d_%d" % (r, b), align_bytes=64)
            scaled.setdefault((r, b), tile)
            nc.scalar.activation(tile[:], turned[r, b], COPY, scale=gate_cols[r][:, b : b + 1])

        def turn_back(t0, n):
            bank_tile = psum.tile([P, n], F32, name="back%d" % t0, tag=free_banks.pop(0))
            back.setdefault(t0, bank_tile)
            for a in range(0, n, P):
                b = (t0 + a) // P
                rs = [r for r in (2, 3) if (r, b) in scaled]
                for r in rs:
                    nc.tensor.matmul(
                        bank_tile[:, a : a + P],
                        lhsT=scaled[r, b][:],
                        rhs=ident[:],
                        start=(r == rs[0]),
                        stop=(r == rs[-1]),
                        is_transpose=True,
                    )

        def fetch_gated(r, t0, n):
            nc.vector.tensor_tensor(
                prod[:, r, t0 : t0 + n],
                y[:].indirect(pos_sb[r][:, t0 // 16 : (t0 + n) // 16]),
                gates[:, r, t0 : t0 + n],
                MULT,
            )

        def add_parts(t0, n):
            nc.vector.tensor_tensor(part[:, t0 : t0 + n], prod[:, 0, t0 : t0 + n], prod[:, 1, t0 : t0 + n], ADD)

        def finish(t0, n, sums):
            nc.vector.tensor_tensor(res[:, t0 : t0 + n], back[t0][:], sums, ADD)
            nc.sync.dma_start(out[:, t0 : t0 + n], res[:, t0 : t0 + n])

        fetch_plain(2, 0, 256)
        fetch_plain(3, 0, 384)
        fetch_plain(2, 256, 384)
        for r in (2, 3):
            for b in (0, 1):
                scale(r, b)
        turn_back(0, 256)
        for b in (3, 4):
            scale(2, b)
        turn_back(384, 256)
        for r in (3, 2):
            scale(r, 2)
        turn_back(256, 128)

        nc.vector.tensor_tensor(prod_last[:], y[:].indirect(pos_sb[3][:, (T - 2 * P) // 16 : T // 16]), gate_last[:], MULT)
        fetch_gated(0, 0, T)
        fetch_gated(1, 0, T)
        nc.vector.tensor_tensor(half_last[:], prod_last[:], prod[:, 0, T - 2 * P : T], ADD)
        add_parts(0, 384)
        nc.vector.tensor_tensor(part[:, T - 2 * P : T], half_last[:], prod[:, 1, T - 2 * P : T], ADD)
        for t0, n in ((0, 256), (384, 256), (256, 128)):
            finish(t0, n, part[:, t0 : t0 + n])
